import numpy as np
CORES = [6,14,22,30,38,46,54,62,134,142,150,158,166,174,182,190,262,270,278,286,294,302,310,318,390,398,406,414,422,430,438,446]
N = 32
T, K = 256, 3
ROUTE = [[[31,24,1],[25,17,13],[5,28,10],[4,27,31],[28,9,20],[16,28,14],[29,24,22],[31,28,12],[15,20,4],[4,26,15],[31,24,11],[13,20,29],[17,12,22],[10,7,31],[28,21,23],[27,4,23],[0,5,4],[4,26,1],[28,10,25],[9,2,28],[15,27,23],[31,17,27],[4,29,27],[2,12,6],[30,21,29],[30,8,0],[5,2,19],[0,28,24],[2,24,18],[6,15,8],[19,17,9],[3,27,28],[18,5,1],[4,28,18],[25,9,6],[10,30,15],[18,11,15],[9,12,28],[15,9,17],[4,21,16],[12,25,23],[25,10,12],[6,28,26],[8,2,27],[9,7,11],[9,22,8],[5,24,21],[28,18,19],[16,7,25],[9,14,28],[11,29,3],[28,8,24],[29,30,14],[5,11,25],[19,17,24],[17,27,23],[13,0,17],[28,4,9],[20,9,1],[3,14,1],[7,31,18],[16,1,14],[19,7,5],[0,29,20],[7,22,26],[10,28,2],[29,0,27],[4,16,7],[25,2,8],[25,27,13],[18,20,21],[28,7,1],[18,3,0],[30,20,4],[9,7,1],[30,17,4],[4,5,12],[26,19,17],[17,2,22],[8,18,25],[1,26,31],[6,23,16],[30,15,12],[1,9,20],[28,21,4],[6,18,20],[16,26,31],[2,15,23],[21,12,7],[6,27,23],[1,7,12],[1,11,19],[29,4,8],[0,24,6],[28,30,27],[5,12,25],[29,31,14],[20,26,16],[31,23,2],[6,9,3],[7,10,13],[6,25,27],[22,2,14],[13,22,10],[0,31,6],[26,16,5],[10,7,18],[30,20,5],[27,17,1],[18,14,27],[17,20,12],[1,20,16],[25,30,31],[4,5,10],[23,1,21],[27,7,29],[10,7,20],[19,12,30],[10,13,24],[6,27,18],[25,7,4],[28,13,17],[3,15,30],[18,23,4],[22,0,3],[16,15,17],[30,23,1],[2,9,3],[20,7,10],[4,20,15],[2,7,25],[10,6,18],[7,4,5],[28,29,25],[11,25,7],[4,20,24],[22,2,10],[12,31,0],[4,28,20],[11,27,12],[7,15,17],[1,21,20],[19,1,28],[9,13,12],[21,8,31],[21,2,6],[2,30,31],[23,2,22],[27,14,2],[0,9,15],[3,13,28],[10,28,23],[6,25,1],[8,21,26],[25,22,0],[0,17,8],[13,28,15],[8,13,26],[26,27,4],[29,15,22],[8,13,29],[18,4,7],[23,2,21],[19,4,31],[12,19,0],[21,11,16],[3,19,22],[14,2,17],[2,18,30],[28,27,9],[8,30,24],[31,27,19],[4,11,2],[28,4,20],[29,23,0],[12,7,10],[23,11,27],[27,5,8],[21,29,27],[21,31,1],[1,10,15],[26,12,24],[7,11,3],[4,7,13],[28,1,24],[20,14,8],[14,7,28],[14,20,30],[11,24,0],[4,15,21],[28,13,2],[4,0,26],[1,22,29],[2,10,9],[18,23,19],[26,23,27],[25,31,17],[5,23,7],[17,19,14],[27,30,4],[7,2,5],[29,1,17],[9,1,11],[6,19,5],[12,20,26],[15,4,21],[21,26,23],[7,16,5],[16,29,11],[28,16,17],[8,17,19],[17,1,30],[0,7,10],[9,28,0],[22,27,12],[3,8,28],[13,2,5],[15,17,20],[30,22,10],[6,12,2],[4,29,7],[13,22,15],[23,8,6],[15,4,26],[17,30,8],[23,16,21],[0,19,27],[12,30,19],[6,5,7],[18,15,26],[0,30,16],[26,31,21],[29,30,25],[18,2,4],[8,4,31],[30,0,3],[18,24,14],[8,11,21],[21,23,22],[31,14,1],[17,14,7],[26,8,14],[17,0,7],[25,7,10],[30,0,5],[5,7,29],[23,27,16],[22,26,16],[15,1,13],[15,3,9],[26,27,24],[7,8,21],[6,4,15],[29,31,26],[28,14,15],[27,3,8]],[[16,9,28],[26,22,25],[20,14,12],[18,4,2],[30,21,15],[24,15,5],[5,14,7],[0,20,3],[24,28,21],[17,16,0],[4,7,6],[22,2,13],[7,21,22],[26,11,1],[12,27,16],[13,0,15],[11,20,18],[26,12,14],[17,4,6],[31,29,21],[22,27,10],[23,20,11],[8,16,13],[21,7,15],[31,5,3],[9,4,25],[27,12,11],[6,1,25],[19,24,30],[1,23,2],[6,15,17],[21,3,31],[22,30,11],[1,30,23],[12,3,24],[31,26,22],[5,11,29],[14,19,18],[8,7,10],[3,30,10],[29,12,26],[18,26,31],[12,20,31],[30,26,28],[29,2,14],[29,15,20],[0,16,21],[0,10,3],[10,29,22],[6,26,16],[6,16,19],[26,9,16],[31,28,1],[10,21,28],[5,9,27],[10,4,20],[0,21,17],[10,30,12],[14,28,12],[23,20,13],[18,13,5],[0,3,25],[28,4,31],[28,9,27],[16,29,10],[5,28,0],[28,7,23],[15,29,2],[10,9,26],[0,15,9],[22,5,26],[14,13,16],[14,26,2],[2,1,12],[27,21,18],[25,24,5],[4,3,1],[11,6,30],[9,7,26],[5,26,14],[5,23,8],[2,16,18],[26,1,11],[25,29,18],[10,20,16],[27,7,0],[24,5,7],[5,17,31],[10,6,23],[25,11,2],[31,9,8],[1,24,9],[20,1,23],[14,20,17],[2,25,0],[17,21,14],[18,10,17],[15,26,16],[8,13,31],[10,4,28],[12,10,31],[27,15,11],[17,15,1],[13,16,23],[31,7,15],[3,21,1],[26,5,12],[3,28,14],[26,29,14],[0,23,30],[5,14,9],[25,14,8],[11,30,19],[2,7,22],[22,4,14],[18,31,10],[10,12,30],[1,16,19],[22,9,27],[8,6,13],[30,15,6],[15,4,12],[20,24,12],[20,24,28],[22,28,18],[3,9,17],[8,18,28],[27,18,20],[5,26,30],[10,20,27],[3,7,11],[15,27,28],[13,9,18],[21,17,26],[5,31,30],[9,5,6],[16,19,24],[19,10,9],[5,0,7],[3,17,21],[0,19,30],[15,1,14],[14,23,28],[11,30,0],[30,21,28],[18,28,29],[0,20,28],[3,17,10],[29,15,23],[26,25,9],[6,29,3],[1,12,10],[13,11,25],[1,0,21],[19,15,0],[1,3,19],[9,16,0],[11,6,31],[2,26,14],[10,3,25],[28,12,11],[6,24,22],[4,11,16],[1,31,8],[12,4,22],[9,11,3],[17,6,22],[31,4,28],[10,15,21],[28,15,30],[17,3,6],[13,25,2],[26,0,23],[21,2,0],[10,3,29],[6,27,2],[11,26,21],[26,12,4],[10,5,24],[8,28,10],[26,16,10],[25,0,15],[18,13,12],[24,9,8],[24,19,9],[8,16,4],[30,4,3],[17,6,30],[25,21,27],[19,16,17],[11,26,5],[13,16,5],[9,11,23],[16,18,6],[26,16,10],[19,13,0],[25,2,5],[16,30,28],[12,10,30],[27,10,3],[20,29,22],[2,30,27],[26,23,8],[5,26,31],[16,30,0],[7,0,12],[30,31,14],[30,12,11],[8,5,14],[23,15,12],[7,25,27],[28,6,8],[20,30,4],[23,27,15],[12,23,7],[31,10,4],[3,14,26],[19,10,3],[20,31,25],[9,15,7],[21,0,16],[26,0,19],[18,13,24],[30,18,21],[20,16,3],[0,21,5],[15,19,24],[31,17,7],[0,3,10],[26,22,29],[17,21,8],[15,6,11],[23,14,18],[1,5,0],[30,9,13],[16,27,0],[18,17,2],[21,12,6],[20,6,2],[26,1,16],[4,14,11],[31,15,6],[27,20,8],[28,14,2],[1,8,6],[21,19,24],[3,17,8],[4,0,22],[7,18,4],[10,17,14],[26,16,19],[20,16,17],[0,9,3],[25,18,10],[27,26,28],[26,24,27]],[[5,10,11],[10,16,15],[4,5,2],[29,19,24],[28,8,12],[23,0,26],[17,29,12],[26,16,9],[20,0,14],[30,29,2],[27,25,2],[8,29,19],[25,27,16],[28,13,18],[26,21,16],[1,3,17],[26,12,28],[23,1,25],[22,31,23],[22,1,21],[4,20,29],[31,29,3],[0,16,24],[3,8,13],[3,23,12],[4,30,9],[9,30,8],[31,19,20],[31,11,3],[16,27,29],[21,20,31],[27,22,20],[0,7,1],[15,11,30],[31,2,18],[28,2,4],[27,25,0],[17,29,3],[19,2,18],[27,3,26],[22,16,17],[17,24,31],[11,8,17],[8,1,4],[29,1,4],[1,31,5],[14,29,11],[27,18,0],[9,29,12],[4,16,27],[7,0,8],[15,4,25],[26,8,7],[13,8,29],[27,11,17],[23,2,5],[30,21,4],[14,30,20],[5,22,2],[9,15,16],[12,16,24],[4,25,9],[9,31,15],[10,21,13],[25,1,12],[16,2,23],[28,1,12],[14,31,19],[20,11,13],[8,10,13],[7,26,20],[6,8,2],[16,10,19],[24,5,19],[22,27,31],[21,8,1],[30,16,0],[5,19,3],[27,0,23],[27,30,22],[5,13,16],[10,1,30],[12,30,17],[16,26,6],[27,19,18],[28,23,13],[28,15,21],[29,11,24],[28,21,19],[29,11,4],[20,27,22],[10,16,27],[24,1,10],[2,19,23],[23,12,20],[8,31,19],[15,12,27],[8,26,19],[24,27,7],[7,19,25],[21,12,22],[12,4,18],[27,8,7],[27,22,19],[17,12,11],[2,24,6],[4,9,0],[8,3,29],[7,11,1],[15,20,6],[15,5,11],[6,5,7],[20,14,21],[3,7,10],[15,23,31],[4,7,29],[19,31,5],[30,4,22],[30,23,4],[30,11,28],[8,12,21],[27,7,8],[19,22,10],[30,9,23],[13,18,29],[29,26,2],[19,30,8],[25,17,12],[14,3,15],[19,21,10],[27,4,0],[6,1,21],[4,6,29],[17,6,7],[0,26,15],[13,7,30],[5,12,15],[13,7,31],[0,29,6],[11,31,29],[1,20,29],[31,6,12],[27,16,21],[1,16,20],[27,6,20],[19,10,3],[13,19,29],[1,10,30],[3,28,7],[16,22,13],[29,8,11],[17,3,22],[31,12,10],[27,26,17],[7,27,25],[29,6,1],[22,10,19],[4,6,5],[20,3,23],[28,7,21],[19,11,12],[10,3,25],[2,20,25],[27,11,5],[27,5,22],[8,15,5],[24,21,2],[14,25,6],[31,6,12],[20,9,24],[3,25,2],[4,7,6],[6,29,4],[28,12,23],[13,23,12],[11,5,12],[5,29,18],[15,5,2],[21,2,3],[31,11,25],[21,15,12],[2,7,8],[11,17,30],[1,6,23],[3,14,0],[24,3,30],[8,15,12],[8,1,24],[17,22,24],[14,0,21],[0,12,20],[11,12,19],[1,8,20],[20,31,21],[3,24,18],[15,28,4],[21,17,10],[5,13,20],[12,18,24],[26,10,1],[12,7,18],[22,20,31],[4,22,21],[3,12,10],[27,15,28],[10,13,1],[11,10,20],[7,6,29],[20,1,16],[21,9,14],[4,12,13],[21,20,16],[23,16,4],[23,2,1],[12,8,6],[1,18,11],[5,31,1],[27,0,15],[30,13,16],[23,16,30],[13,17,25],[28,30,15],[23,11,21],[25,5,1],[13,18,30],[24,7,8],[12,27,19],[17,7,8],[2,28,16],[17,0,27],[17,12,6],[18,10,25],[3,17,12],[28,31,23],[20,28,16],[25,14,24],[5,3,18],[28,7,4],[7,16,21],[28,10,1],[16,15,22],[26,22,8],[14,29,11],[13,19,27],[23,3,30],[31,17,8],[24,27,6],[23,14,15],[10,4,16],[10,22,21],[24,3,28],[7,21,11],[7,10,4],[29,24,13],[26,0,8],[12,31,1]],[[24,2,1],[27,25,13],[27,7,29],[19,0,25],[4,3,12],[5,27,8],[0,14,15],[9,29,24],[3,15,2],[4,7,10],[21,8,31],[20,8,29],[23,16,25],[4,26,19],[26,15,31],[21,5,8],[17,23,3],[20,0,24],[17,22,18],[24,15,12],[4,31,29],[20,29,25],[22,21,6],[8,16,13],[16,8,18],[14,9,10],[0,27,4],[26,28,2],[21,8,10],[26,10,13],[1,27,7],[29,0,15],[6,10,28],[8,29,31],[13,4,12],[28,23,17],[3,16,13],[27,21,29],[12,31,15],[19,18,3],[26,23,17],[0,25,26],[22,7,11],[14,13,2],[12,20,16],[29,5,26],[15,5,30],[11,21,25],[11,10,28],[12,26,25],[8,31,7],[26,14,1],[4,5,3],[31,19,26],[17,23,25],[6,18,20],[13,12,27],[0,6,25],[12,2,20],[8,23,18],[25,17,15],[14,10,2],[13,0,30],[26,18,20],[14,6,4],[6,13,19],[22,21,29],[26,13,8],[31,29,18],[3,10,28],[15,17,18],[7,24,18],[24,28,30],[8,31,26],[22,19,6],[8,5,23],[14,27,28],[11,20,1],[0,19,25],[5,6,2],[15,9,30],[3,13,5],[31,11,20],[24,10,8],[16,5,2],[13,5,19],[10,27,11],[16,13,30],[1,6,2],[27,28,0],[13,9,27],[16,25,5],[23,16,11],[17,25,31],[27,4,16],[2,21,27],[25,2,16],[1,19,2],[15,26,13],[6,31,15],[1,23,12],[25,10,16],[25,6,18],[26,3,28],[20,2,24],[20,11,13],[24,9,3],[17,12,19],[29,25,7],[16,14,13],[2,29,3],[11,6,0],[14,30,16],[28,31,21],[7,24,16],[13,17,14],[24,23,28],[20,0,25],[2,26,1],[22,15,31],[2,25,0],[9,7,18],[13,28,3],[11,30,16],[4,19,13],[30,11,14],[6,26,23],[17,8,6],[0,15,14],[16,13,29],[24,27,11],[13,20,4],[27,15,8],[0,28,17],[27,21,12],[21,2,4],[12,30,9],[29,18,17],[2,30,12],[6,12,15],[9,6,3],[12,19,10],[12,7,11],[27,25,5],[9,27,17],[1,30,31],[8,16,13],[10,28,7],[5,13,29],[30,8,11],[28,3,25],[25,6,10],[1,13,2],[22,24,7],[15,20,17],[27,0,16],[8,22,14],[30,20,17],[16,1,14],[22,15,30],[25,10,9],[24,14,1],[14,16,6],[6,18,26],[17,21,5],[2,0,3],[9,18,24],[17,26,12],[29,27,12],[16,27,26],[26,23,24],[4,16,29],[26,8,29],[14,22,0],[24,28,10],[14,17,3],[11,7,6],[23,2,15],[5,6,29],[22,10,23],[19,7,31],[2,28,12],[13,2,22],[9,17,7],[20,13,8],[30,13,0],[5,11,9],[23,13,27],[6,30,31],[2,22,26],[29,25,7],[8,25,2],[12,11,2],[3,21,5],[30,2,24],[26,25,8],[22,28,16],[29,3,30],[24,1,13],[1,27,30],[22,27,21],[12,0,13],[4,13,8],[11,9,26],[4,11,8],[24,26,15],[12,16,1],[12,24,5],[20,13,30],[22,11,23],[30,28,25],[17,10,2],[30,13,4],[10,19,13],[5,31,4],[23,1,31],[10,2,18],[23,12,3],[28,13,8],[25,20,24],[6,16,14],[24,2,29],[1,30,2],[11,17,27],[27,17,5],[26,0,21],[2,5,23],[26,5,10],[19,14,13],[5,24,7],[18,28,13],[30,14,25],[25,6,21],[14,18,23],[14,31,11],[23,17,16],[30,2,8],[6,17,13],[1,21,30],[25,16,22],[29,27,18],[7,29,1],[20,26,14],[27,28,22],[29,4,2],[5,3,2],[4,22,30],[2,31,22],[15,8,21],[2,15,14],[12,6,13],[30,8,9],[4,15,31],[0,27,23],[5,22,16],[21,6,23]],[[23,31,12],[18,25,3],[22,29,26],[23,15,1],[12,21,31],[6,3,24],[2,5,9],[25,12,5],[7,1,23],[20,13,7],[10,17,20],[30,4,24],[18,29,15],[19,30,4],[30,0,23],[23,25,4],[26,18,8],[31,2,14],[6,17,20],[9,1,16],[7,18,23],[18,25,7],[24,20,22],[11,19,23],[4,11,24],[13,27,12],[19,26,23],[1,26,6],[3,25,4],[30,0,7],[6,18,4],[27,15,26],[7,28,22],[26,1,21],[21,25,14],[8,7,31],[30,24,0],[23,9,30],[3,22,24],[26,23,31],[31,29,26],[15,12,0],[5,22,17],[12,8,1],[12,22,25],[19,2,31],[22,23,6],[14,12,22],[26,13,11],[21,29,30],[11,2,30],[29,17,7],[2,31,27],[12,7,17],[8,12,18],[11,2,4],[25,11,0],[29,1,31],[8,24,7],[0,25,26],[5,16,6],[21,30,12],[9,5,19],[22,13,20],[30,17,9],[4,29,30],[22,24,9],[29,20,6],[29,17,30],[25,22,13],[10,28,27],[21,23,25],[29,22,4],[18,22,12],[19,6,20],[18,13,3],[10,16,19],[11,8,10],[10,1,28],[4,25,15],[5,29,12],[31,5,17],[7,30,19],[17,14,28],[6,10,24],[27,6,9],[10,18,28],[24,19,4],[26,30,0],[1,18,16],[27,17,28],[28,7,1],[15,16,9],[10,30,3],[26,0,29],[12,0,8],[0,17,10],[2,31,26],[16,27,28],[20,12,13],[1,18,29],[16,12,15],[6,5,3],[12,14,30],[19,24,18],[22,25,26],[15,24,8],[10,21,11],[23,1,28],[16,25,23],[1,11,28],[14,29,12],[4,13,0],[5,28,2],[13,3,30],[14,0,21],[23,25,17],[23,29,16],[18,12,6],[0,27,30],[7,21,20],[15,0,21],[15,18,11],[3,30,1],[29,17,23],[6,28,9],[25,26,13],[24,19,14],[8,14,0],[31,25,30],[19,10,26],[5,19,30],[14,21,7],[27,30,11],[17,5,15],[9,11,15],[9,3,5],[25,9,5],[23,18,2],[25,8,0],[17,20,8],[29,20,10],[4,3,8],[2,20,0],[12,22,2],[17,7,14],[30,0,10],[5,18,28],[1,0,29],[18,23,3],[26,6,3],[31,20,6],[12,8,1],[28,6,26],[21,25,24],[25,2,29],[10,0,8],[11,10,2],[9,10,19],[3,6,19],[13,22,6],[30,23,18],[2,0,15],[10,30,19],[24,10,19],[13,20,28],[11,1,4],[0,24,30],[2,16,23],[6,3,2],[10,12,11],[8,9,29],[7,22,4],[13,21,4],[8,14,28],[22,18,11],[29,8,11],[14,19,18],[17,20,9],[10,26,13],[12,30,1],[1,14,26],[3,23,7],[4,5,6],[19,30,13],[5,17,23],[9,30,21],[18,2,16],[8,14,11],[20,5,28],[15,9,8],[1,23,2],[31,4,22],[23,0,17],[10,17,16],[21,10,2],[15,14,31],[9,16,25],[5,21,0],[30,8,27],[3,0,23],[28,10,24],[11,12,6],[19,17,30],[19,22,27],[24,4,18],[16,1,30],[20,25,16],[14,20,25],[31,18,0],[17,29,12],[20,16,8],[26,18,0],[29,8,27],[1,5,14],[16,23,22],[15,20,29],[7,26,28],[4,18,0],[3,27,30],[6,2,29],[5,0,2],[5,0,7],[23,14,11],[3,7,24],[21,5,24],[6,0,14],[11,23,12],[28,10,5],[10,22,15],[18,27,15],[31,12,0],[17,30,22],[3,8,26],[3,26,6],[24,4,9],[11,16,26],[18,7,23],[21,5,1],[3,0,17],[22,28,26],[2,1,31],[24,2,1],[18,7,21],[10,22,31],[1,17,4],[12,7,21],[31,10,4],[2,30,14],[17,11,14],[28,6,4],[9,31,6],[27,15,23],[11,4,15],[26,31,12],[4,30,20]],[[8,11,12],[2,5,0],[9,31,26],[7,15,23],[4,10,20],[9,22,12],[5,27,9],[13,3,15],[12,31,0],[10,14,15],[22,28,12],[15,5,22],[31,10,21],[15,27,7],[26,25,9],[5,19,26],[7,28,12],[22,25,1],[13,21,12],[20,18,6],[22,9,8],[24,16,6],[11,0,31],[16,26,13],[24,13,27],[10,1,6],[11,4,21],[4,10,15],[0,11,22],[22,7,14],[17,2,14],[10,28,29],[11,13,3],[21,11,0],[19,5,8],[25,5,29],[7,20,9],[5,25,12],[0,21,7],[8,18,28],[2,29,7],[17,18,13],[19,11,4],[16,15,27],[1,30,20],[3,11,2],[0,3,12],[29,14,5],[20,11,3],[7,28,5],[23,28,31],[18,7,13],[6,1,26],[7,4,16],[31,1,24],[24,0,28],[2,31,25],[25,20,8],[8,5,16],[28,3,4],[3,19,7],[13,6,21],[4,31,19],[28,23,1],[22,13,21],[19,24,31],[0,18,13],[19,28,31],[30,13,8],[5,3,16],[15,26,18],[29,11,18],[10,16,6],[27,16,0],[22,15,3],[7,20,22],[29,24,17],[25,24,5],[3,22,15],[0,8,15],[27,1,11],[30,5,22],[19,18,15],[22,25,2],[14,30,20],[18,13,24],[12,22,3],[23,19,13],[24,1,13],[10,19,22],[2,30,0],[31,9,13],[15,17,8],[3,4,28],[2,29,10],[27,29,21],[11,13,5],[5,30,21],[24,11,30],[21,27,12],[12,29,23],[23,26,10],[28,3,0],[18,20,26],[15,18,1],[12,6,18],[8,2,19],[5,25,9],[9,31,22],[16,6,5],[1,12,19],[26,30,28],[30,4,26],[30,21,25],[16,28,24],[10,28,2],[22,5,0],[16,21,5],[6,19,1],[11,1,10],[6,18,8],[12,16,15],[21,12,10],[25,17,6],[2,18,25],[8,12,17],[30,15,13],[4,2,14],[1,28,12],[18,14,7],[2,27,15],[7,13,26],[6,28,15],[19,6,21],[18,23,0],[28,1,12],[14,24,27],[16,10,4],[7,14,6],[17,26,22],[23,1,11],[3,7,11],[14,2,17],[16,14,5],[11,27,18],[17,22,23],[2,15,0],[21,5,2],[3,22,7],[15,30,16],[16,23,0],[26,3,22],[27,0,28],[24,29,15],[0,3,10],[4,30,22],[0,22,20],[9,3,19],[0,10,5],[14,1,31],[15,27,22],[24,5,22],[24,5,0],[31,3,9],[19,31,14],[10,29,17],[20,5,16],[9,10,8],[6,7,24],[29,22,3],[15,10,20],[15,20,24],[7,25,10],[8,5,1],[9,10,19],[15,14,22],[12,3,23],[3,7,1],[26,14,22],[28,30,29],[18,1,20],[13,11,29],[26,31,27],[13,8,25],[22,26,18],[2,8,12],[10,26,15],[10,14,16],[14,1,20],[0,3,16],[26,24,17],[27,10,6],[4,14,8],[15,0,14],[29,27,24],[14,15,28],[29,18,2],[23,13,29],[15,22,4],[12,23,19],[10,6,7],[20,8,29],[17,31,3],[26,2,23],[11,3,26],[23,26,18],[31,5,24],[10,31,1],[24,11,29],[26,0,13],[6,31,10],[24,29,4],[28,0,26],[12,10,22],[20,16,10],[21,14,7],[17,31,29],[6,22,7],[6,14,3],[23,17,0],[18,13,22],[15,31,14],[26,7,27],[21,0,1],[27,21,13],[20,31,16],[29,1,11],[25,4,5],[25,11,28],[18,25,3],[12,10,17],[22,15,4],[13,28,20],[28,9,3],[17,15,29],[28,17,27],[28,18,15],[25,23,24],[9,26,10],[8,2,18],[8,14,19],[29,18,24],[24,29,21],[23,11,31],[6,25,21],[18,16,20],[18,8,2],[16,6,7],[4,0,7],[24,27,29],[18,16,10],[9,0,10],[11,12,21],[27,20,21],[10,30,6],[21,24,9]],[[1,18,23],[17,9,27],[8,13,20],[13,21,25],[21,16,9],[11,4,15],[20,13,25],[21,19,1],[18,13,3],[2,12,27],[7,14,18],[22,21,28],[24,13,17],[14,3,15],[2,15,6],[29,0,24],[12,5,15],[28,15,13],[29,28,7],[27,9,1],[9,1,26],[26,27,23],[17,27,10],[5,28,11],[18,24,16],[6,24,4],[24,21,26],[19,6,12],[23,15,18],[16,31,3],[24,14,26],[6,26,28],[11,10,18],[3,1,4],[28,16,29],[23,29,10],[24,12,27],[3,28,18],[3,5,30],[29,12,1],[11,18,22],[12,10,16],[18,8,24],[7,0,15],[27,4,17],[1,7,19],[27,1,19],[13,19,3],[27,25,1],[8,16,6],[4,3,10],[29,15,20],[30,0,9],[26,6,16],[6,24,1],[6,0,23],[8,12,21],[31,1,29],[20,23,9],[20,17,31],[29,4,21],[22,12,14],[28,22,4],[28,19,14],[19,10,0],[3,1,31],[3,5,0],[18,23,8],[7,4,11],[12,28,14],[26,8,30],[25,0,20],[18,20,15],[15,26,16],[19,20,12],[1,15,4],[1,30,4],[3,19,11],[22,2,18],[5,4,13],[29,18,0],[12,5,3],[13,3,2],[2,23,5],[10,1,27],[6,26,27],[15,2,14],[23,16,18],[2,1,23],[26,28,4],[9,22,19],[11,9,25],[11,7,0],[12,14,15],[8,10,21],[14,11,23],[9,12,28],[30,6,20],[12,27,14],[9,27,1],[5,19,26],[16,2,19],[12,22,0],[20,25,2],[17,1,22],[22,31,5],[26,22,14],[29,16,19],[30,17,16],[11,20,18],[24,12,0],[31,15,1],[20,11,21],[6,16,12],[6,13,8],[8,6,1],[30,5,12],[1,6,16],[27,11,4],[29,9,30],[29,30,9],[13,30,4],[18,12,26],[0,4,2],[1,20,2],[13,29,16],[9,7,21],[12,0,31],[30,19,5],[6,25,9],[8,10,24],[29,5,28],[18,10,11],[10,11,21],[12,25,16],[6,5,28],[4,3,27],[30,25,11],[30,27,25],[4,3,5],[12,13,10],[23,30,0],[16,21,30],[3,26,15],[20,13,31],[31,14,28],[31,8,11],[24,11,8],[8,23,4],[20,26,7],[8,26,31],[15,21,30],[23,9,8],[3,12,14],[24,5,0],[5,19,31],[14,31,0],[4,26,22],[27,13,26],[21,7,3],[13,20,1],[0,15,2],[10,28,17],[13,19,18],[23,17,0],[9,17,19],[14,6,21],[23,19,22],[16,8,26],[19,1,22],[10,18,13],[22,8,9],[24,21,12],[11,7,18],[16,10,18],[12,5,21],[20,8,2],[7,15,31],[22,9,20],[11,15,14],[1,29,4],[9,7,1],[6,26,20],[8,18,14],[19,10,27],[25,8,4],[24,26,2],[16,21,18],[24,17,28],[18,12,3],[24,1,19],[29,28,17],[7,27,14],[1,23,27],[24,1,8],[2,3,25],[3,6,23],[16,22,2],[10,24,15],[11,12,18],[28,21,3],[22,0,20],[20,27,5],[25,26,1],[17,2,23],[18,7,24],[15,23,28],[12,22,26],[10,26,25],[3,23,31],[18,31,11],[15,10,26],[20,7,24],[25,14,20],[4,26,25],[7,2,13],[10,0,11],[10,29,2],[5,4,1],[20,25,26],[2,20,24],[26,6,27],[5,27,22],[4,14,28],[22,8,17],[13,10,12],[6,5,19],[22,3,6],[10,16,7],[5,20,6],[20,15,14],[15,17,18],[12,13,29],[24,15,30],[25,19,22],[18,17,0],[15,9,12],[0,11,9],[18,2,6],[27,15,19],[16,4,20],[17,24,31],[5,2,6],[29,15,26],[4,7,17],[22,17,24],[24,0,8],[20,2,6],[13,3,30],[25,1,20],[7,4,12],[26,17,4],[27,29,1],[24,18,22],[26,15,27],[23,6,21]],[[3,9,23],[29,4,31],[11,19,18],[15,6,16],[3,5,20],[11,22,14],[25,12,1],[11,8,18],[15,10,22],[12,0,2],[15,29,20],[9,6,5],[22,28,3],[21,7,12],[8,0,21],[29,9,6],[13,28,31],[12,20,9],[23,2,30],[10,3,26],[18,13,7],[3,23,8],[24,13,5],[11,23,24],[5,29,25],[15,22,1],[30,31,13],[8,26,0],[30,5,31],[19,13,2],[24,9,22],[13,18,5],[2,6,19],[22,25,13],[23,0,7],[12,23,26],[18,26,12],[20,0,29],[2,17,13],[21,20,18],[4,16,13],[22,8,29],[23,17,25],[11,4,5],[21,16,8],[4,11,24],[8,23,19],[1,18,17],[23,25,10],[31,19,9],[15,17,19],[1,28,12],[27,19,18],[0,18,10],[19,18,0],[28,9,14],[18,27,22],[15,31,29],[29,18,2],[24,29,8],[19,25,12],[26,14,10],[17,29,3],[25,3,9],[27,10,24],[27,31,19],[24,26,5],[27,30,2],[23,31,1],[7,4,3],[20,2,29],[25,10,30],[20,3,27],[10,16,7],[20,4,21],[29,15,27],[13,1,25],[21,14,22],[7,13,22],[13,14,19],[13,23,22],[18,7,22],[5,15,24],[24,1,12],[30,29,27],[0,14,3],[1,28,8],[26,20,23],[9,28,8],[17,18,31],[12,2,9],[27,8,3],[27,18,29],[29,11,0],[4,1,3],[9,0,31],[2,14,29],[14,7,23],[1,24,5],[17,8,1],[17,24,22],[7,8,16],[15,31,24],[31,12,18],[6,19,20],[4,27,0],[17,2,25],[10,21,26],[30,10,0],[11,3,30],[12,21,14],[7,13,20],[26,18,1],[16,23,14],[8,15,9],[14,1,8],[28,4,9],[12,17,7],[26,15,0],[15,24,10],[27,21,14],[19,2,0],[7,30,28],[20,30,18],[6,5,4],[15,16,17],[11,26,31],[1,30,7],[25,10,4],[20,28,14],[23,30,1],[21,18,2],[26,17,0],[26,13,9],[13,16,0],[1,17,21],[1,29,23],[7,23,5],[0,11,31],[19,31,15],[26,11,12],[4,1,30],[18,15,6],[7,2,9],[27,3,7],[29,27,30],[13,27,3],[12,0,16],[3,18,14],[24,5,4],[17,22,28],[24,3,15],[28,8,6],[4,24,23],[2,21,12],[30,6,8],[17,4,5],[7,23,18],[10,2,27],[19,30,16],[8,27,2],[31,24,3],[28,6,30],[6,22,14],[5,24,21],[2,19,31],[23,26,21],[22,25,12],[2,19,28],[14,7,21],[28,3,16],[9,0,21],[18,31,30],[14,26,0],[5,26,23],[19,8,1],[24,22,15],[10,11,9],[16,10,1],[26,2,6],[5,6,10],[2,30,17],[10,2,5],[23,0,10],[20,7,9],[30,22,19],[22,11,28],[29,6,12],[15,17,4],[19,6,11],[16,8,19],[28,3,1],[17,9,1],[26,14,0],[24,15,28],[15,3,7],[27,2,31],[12,18,13],[28,18,6],[5,8,18],[7,2,1],[31,23,26],[19,9,2],[18,27,22],[9,31,20],[19,27,7],[13,22,12],[21,12,29],[12,28,7],[5,1,28],[22,17,31],[13,1,0],[29,9,11],[8,3,16],[16,4,3],[15,26,12],[24,28,7],[28,22,16],[3,10,29],[1,13,20],[27,9,0],[25,0,29],[30,0,3],[21,8,14],[10,31,4],[20,7,22],[8,14,9],[11,27,4],[7,14,23],[21,12,23],[17,31,4],[0,8,9],[8,11,26],[8,27,2],[17,19,20],[24,27,7],[25,1,23],[20,9,5],[11,23,25],[22,9,4],[17,8,1],[27,8,17],[15,18,7],[3,31,26],[20,10,17],[24,17,15],[20,6,15],[2,16,21],[5,17,31],[0,13,7],[1,22,11],[27,8,26],[30,24,4],[23,15,28],[20,10,2],[5,1,4]],[[14,3,20],[10,22,23],[12,16,11],[11,23,22],[22,15,23],[8,18,4],[7,13,1],[14,28,6],[21,14,16],[25,28,15],[26,5,6],[2,9,7],[3,24,19],[8,11,25],[11,14,24],[5,2,20],[22,27,15],[12,21,5],[22,3,5],[22,5,16],[15,7,26],[10,24,31],[2,11,7],[2,17,22],[16,19,31],[25,20,24],[27,4,31],[9,18,22],[3,5,25],[4,22,2],[9,17,7],[30,5,19],[20,31,9],[9,6,16],[20,14,1],[28,27,14],[29,24,10],[8,16,3],[24,25,27],[21,25,0],[9,26,21],[31,9,11],[14,9,17],[29,23,7],[28,1,31],[11,30,26],[2,12,11],[25,16,7],[17,22,10],[22,0,19],[11,19,10],[15,11,1],[20,30,29],[4,17,19],[3,26,18],[20,7,1],[30,9,29],[8,25,29],[29,17,1],[0,2,31],[18,19,13],[19,29,21],[29,16,13],[16,19,3],[11,14,8],[20,21,16],[18,9,3],[24,2,29],[6,23,29],[3,25,11],[30,2,27],[23,0,18],[31,27,30],[18,8,19],[8,31,5],[10,5,28],[4,27,3],[21,28,8],[20,4,24],[4,11,6],[5,12,21],[9,21,26],[1,2,5],[0,25,18],[13,19,10],[0,24,28],[28,25,17],[18,17,28],[0,24,27],[8,13,29],[23,20,25],[28,15,20],[17,8,15],[28,26,22],[23,5,10],[16,10,14],[1,13,30],[17,15,4],[7,6,3],[26,0,4],[14,1,21],[16,11,2],[10,11,26],[9,28,2],[17,18,15],[24,3,10],[11,23,1],[5,10,31],[18,31,2],[1,26,29],[21,14,4],[9,5,24],[12,31,15],[18,22,12],[15,20,2],[26,9,27],[26,21,30],[1,14,13],[27,19,29],[21,15,13],[21,1,10],[12,1,19],[15,2,26],[5,30,26],[31,14,16],[14,2,9],[31,24,1],[24,9,1],[9,6,10],[5,28,4],[21,13,26],[2,31,17],[31,18,12],[23,12,11],[7,24,30],[31,17,8],[13,7,18],[23,4,8],[30,10,13],[28,22,27],[21,15,13],[30,27,26],[4,0,8],[22,11,0],[20,11,0],[24,28,26],[21,2,15],[8,31,16],[8,0,12],[12,13,8],[15,0,13],[8,6,15],[15,8,11],[27,20,5],[13,26,15],[9,21,25],[30,31,10],[28,11,16],[18,26,28],[12,27,13],[17,10,27],[15,11,29],[30,6,21],[29,3,19],[23,22,8],[15,23,14],[24,8,10],[1,24,7],[26,7,22],[31,18,14],[2,28,19],[20,0,12],[22,27,2],[3,18,25],[28,8,18],[21,4,24],[0,28,7],[16,24,19],[13,27,18],[16,7,9],[15,16,0],[10,4,27],[8,4,13],[26,3,11],[30,23,4],[28,23,24],[5,17,12],[19,13,23],[13,26,31],[29,0,28],[20,3,14],[31,6,8],[0,23,15],[20,15,22],[14,16,22],[1,7,28],[22,8,11],[1,23,14],[28,30,6],[6,16,25],[5,15,24],[26,24,11],[3,10,14],[21,17,10],[18,14,25],[22,30,15],[12,28,10],[27,11,7],[1,22,26],[21,17,29],[12,27,30],[28,24,19],[8,17,23],[22,2,3],[31,20,23],[17,20,6],[27,3,29],[26,3,7],[10,24,26],[7,22,3],[7,27,14],[0,21,19],[10,30,19],[29,14,6],[14,17,23],[13,7,18],[17,21,13],[1,22,20],[31,28,12],[29,26,19],[4,23,21],[19,25,14],[3,21,0],[17,9,14],[9,29,31],[20,28,10],[30,22,12],[7,25,31],[3,21,22],[12,6,24],[0,2,4],[12,25,6],[24,4,18],[31,0,24],[19,16,13],[10,1,8],[7,31,9],[15,28,29],[27,29,2],[4,21,2],[20,25,11],[27,20,31],[3,24,1],[23,31,28],[1,26,15],[21,26,7]],[[23,26,4],[8,24,9],[1,9,0],[18,10,4],[23,26,5],[16,4,13],[13,17,28],[11,13,29],[10,11,22],[17,12,29],[9,20,13],[27,10,26],[20,30,2],[22,25,18],[30,18,8],[18,4,22],[11,8,13],[25,15,0],[23,27,24],[25,8,16],[9,28,31],[6,28,9],[17,25,13],[30,18,6],[7,1,8],[7,14,26],[16,27,25],[18,0,24],[27,25,24],[14,7,29],[5,24,23],[31,24,0],[14,16,20],[11,30,13],[5,14,30],[16,15,24],[26,25,10],[1,16,13],[27,26,18],[8,21,25],[24,13,8],[26,18,15],[4,0,22],[9,27,21],[21,2,17],[12,30,14],[16,19,21],[4,22,3],[3,12,31],[28,25,15],[3,4,23],[25,12,11],[18,12,7],[16,2,10],[19,13,24],[0,11,2],[14,1,25],[4,18,6],[10,9,19],[8,13,30],[9,24,13],[2,30,12],[19,9,4],[20,4,23],[21,29,13],[4,14,2],[29,17,3],[0,20,23],[10,15,17],[24,27,12],[31,27,8],[27,9,16],[31,20,22],[5,6,29],[27,21,23],[25,20,13],[8,0,13],[21,0,31],[23,20,19],[0,17,3],[3,22,15],[13,7,29],[13,29,27],[24,1,11],[10,19,21],[8,12,18],[13,23,14],[0,10,5],[23,16,1],[4,23,2],[4,9,29],[18,4,30],[13,17,9],[17,3,7],[30,31,10],[15,28,18],[2,27,9],[18,5,14],[1,16,27],[12,4,26],[19,4,2],[30,1,19],[6,25,10],[26,17,16],[9,16,5],[16,10,24],[18,1,14],[19,4,0],[24,22,12],[14,23,24],[2,28,31],[30,15,20],[28,9,5],[16,26,4],[19,8,29],[13,9,2],[23,14,18],[29,25,15],[30,18,17],[14,11,25],[9,31,16],[20,9,2],[1,11,23],[30,9,0],[5,2,11],[23,0,10],[25,5,8],[18,30,31],[15,19,24],[5,10,6],[4,7,22],[21,12,4],[1,13,18],[19,6,12],[24,15,6],[29,0,22],[19,4,22],[22,18,0],[23,13,3],[1,11,17],[15,5,31],[17,15,2],[10,4,6],[13,20,25],[5,3,1],[17,7,1],[9,5,12],[27,7,2],[26,30,16],[5,0,8],[16,20,11],[26,22,7],[22,7,6],[12,8,10],[18,20,2],[21,10,4],[6,12,28],[10,1,11],[21,2,7],[10,5,18],[9,11,7],[1,19,18],[4,5,18],[18,8,22],[4,27,26],[0,25,10],[11,17,1],[0,29,10],[8,3,30],[27,21,2],[1,6,22],[4,22,6],[24,18,14],[29,24,16],[23,12,19],[22,20,31],[3,31,26],[21,25,23],[20,3,6],[29,26,18],[13,30,25],[1,12,0],[24,1,23],[22,31,6],[17,14,22],[29,10,19],[10,21,13],[8,23,1],[13,8,14],[9,19,31],[29,10,3],[11,19,24],[30,6,27],[7,8,3],[18,25,17],[1,25,9],[22,16,21],[20,6,12],[22,11,26],[11,21,28],[10,26,5],[4,11,10],[6,5,8],[25,4,9],[28,24,3],[27,9,24],[7,12,17],[10,26,13],[24,9,4],[18,30,0],[24,0,21],[9,12,20],[9,31,2],[28,7,20],[31,30,22],[0,26,9],[3,9,20],[17,29,11],[19,12,20],[29,3,28],[27,25,12],[1,31,14],[23,21,25],[11,12,1],[29,2,17],[8,26,31],[8,25,28],[22,31,12],[15,5,31],[9,1,10],[2,1,10],[25,30,13],[4,0,26],[21,25,30],[13,0,11],[2,30,13],[23,26,28],[1,15,21],[20,14,24],[5,22,17],[21,29,27],[2,18,10],[6,31,20],[13,14,17],[13,15,0],[0,4,18],[23,22,20],[5,21,6],[15,21,28],[28,31,20],[17,3,19],[4,8,2],[19,31,4],[18,4,15],[30,6,4],[8,24,16]],[[11,0,25],[26,31,23],[11,27,22],[20,6,11],[29,27,6],[3,14,10],[31,19,15],[31,10,0],[27,17,22],[15,29,28],[27,15,23],[9,30,7],[9,4,25],[17,19,26],[26,23,21],[12,16,22],[20,16,10],[12,2,11],[12,20,30],[4,26,3],[25,24,23],[23,15,4],[11,3,7],[24,3,7],[21,8,13],[2,12,3],[28,7,6],[22,19,2],[14,24,29],[26,20,14],[16,24,30],[16,12,7],[10,26,24],[0,26,31],[28,14,27],[10,7,2],[8,11,13],[30,4,26],[0,26,16],[10,30,0],[7,4,5],[7,22,31],[13,29,27],[10,23,1],[4,19,26],[17,18,26],[12,7,31],[28,6,2],[9,0,14],[29,20,23],[15,2,29],[12,27,15],[22,15,12],[30,24,12],[14,28,15],[1,14,13],[23,3,7],[14,11,13],[24,10,25],[10,19,12],[10,12,22],[25,0,2],[31,19,13],[12,23,26],[9,25,19],[24,6,15],[30,16,8],[30,24,3],[22,18,9],[26,14,21],[2,13,19],[1,12,10],[30,4,25],[13,8,10],[16,15,21],[12,27,15],[25,23,13],[9,1,20],[3,16,29],[3,20,22],[1,6,31],[26,20,7],[17,13,3],[25,24,19],[21,29,6],[21,15,8],[17,28,26],[10,18,6],[15,8,31],[21,1,27],[0,16,15],[0,16,17],[20,30,19],[16,3,8],[19,4,2],[20,0,3],[1,4,19],[28,18,8],[13,6,0],[12,11,2],[5,30,21],[9,26,13],[7,1,25],[25,27,26],[19,2,12],[6,25,1],[26,0,4],[2,19,25],[14,10,5],[24,4,6],[15,29,23],[19,23,21],[12,4,16],[10,19,25],[16,9,21],[8,30,28],[3,15,29],[31,19,27],[30,22,27],[3,23,18],[14,11,2],[19,18,5],[23,27,7],[2,24,13],[27,4,11],[13,10,27],[22,2,11],[7,9,29],[10,17,20],[15,28,13],[20,7,28],[17,10,1],[9,12,13],[6,15,16],[29,15,3],[24,22,26],[2,30,21],[23,14,12],[19,7,27],[17,6,18],[1,16,24],[24,7,1],[28,26,16],[26,29,4],[8,16,11],[7,8,17],[14,29,3],[21,10,6],[17,0,28],[6,3,27],[0,30,17],[5,16,0],[28,4,8],[23,1,12],[3,26,20],[14,13,7],[26,1,19],[19,24,11],[11,19,13],[16,3,10],[1,9,31],[0,4,30],[25,31,18],[22,26,28],[0,6,17],[23,14,7],[21,6,24],[3,5,4],[13,0,18],[20,21,23],[21,22,14],[1,11,0],[19,24,3],[12,17,31],[0,22,18],[26,22,19],[3,0,7],[4,16,17],[10,21,6],[20,7,14],[29,7,31],[25,14,1],[2,29,3],[23,9,8],[31,4,7],[27,23,1],[25,21,30],[24,25,11],[7,17,15],[2,28,29],[27,12,1],[16,8,13],[0,7,6],[6,0,12],[5,19,28],[10,0,9],[27,16,4],[18,9,6],[26,30,23],[21,18,6],[10,29,6],[1,18,11],[30,5,20],[4,28,14],[19,26,9],[16,17,31],[23,31,25],[25,16,6],[24,4,18],[3,19,31],[18,15,21],[4,24,10],[8,31,27],[16,9,8],[7,9,23],[26,14,7],[2,31,11],[7,29,27],[27,20,1],[20,15,8],[6,14,24],[25,18,27],[6,19,18],[21,2,8],[22,27,11],[2,6,1],[18,15,10],[27,21,24],[21,24,6],[18,9,25],[4,28,27],[2,15,23],[16,26,0],[30,20,29],[17,30,3],[29,0,11],[3,29,24],[20,21,9],[11,26,1],[22,5,21],[9,28,30],[5,16,8],[28,23,16],[7,9,13],[7,27,25],[23,26,24],[13,25,7],[29,21,5],[25,2,31],[12,9,13],[7,23,15],[22,24,26],[25,21,17],[20,31,3],[3,21,26],[4,2,10]],[[2,15,0],[22,24,10],[10,18,7],[21,4,3],[28,22,25],[8,19,9],[9,0,23],[4,28,3],[16,6,0],[20,12,30],[14,22,3],[24,13,6],[17,26,23],[19,18,14],[12,7,2],[26,13,25],[31,2,5],[4,24,1],[2,26,29],[8,3,22],[4,16,3],[23,21,12],[3,11,12],[15,2,16],[0,11,15],[0,1,18],[18,30,22],[4,3,29],[7,1,19],[13,24,30],[6,12,3],[14,0,26],[6,13,14],[15,18,25],[31,30,6],[22,31,3],[22,30,0],[2,12,4],[14,28,25],[24,22,26],[8,22,10],[30,14,20],[2,23,3],[30,4,31],[4,24,30],[19,3,9],[31,12,10],[5,15,21],[17,15,13],[6,15,4],[18,11,25],[30,9,27],[29,0,8],[12,13,26],[18,27,6],[17,0,25],[1,26,16],[19,25,3],[6,25,4],[30,1,3],[5,21,18],[5,14,16],[22,5,31],[16,23,25],[4,0,20],[26,16,6],[7,26,23],[31,9,20],[17,27,26],[7,3,20],[15,27,6],[27,23,10],[30,4,17],[2,18,25],[13,14,31],[24,30,1],[31,7,13],[23,25,16],[29,18,5],[1,24,11],[28,18,30],[6,8,17],[14,2,30],[4,24,7],[11,13,24],[18,9,23],[4,28,30],[15,18,26],[23,21,19],[27,10,29],[5,10,19],[27,22,14],[20,30,16],[17,26,16],[13,1,3],[26,12,4],[23,28,5],[24,7,16],[4,24,23],[25,31,15],[23,7,31],[27,26,7],[4,25,28],[6,0,15],[17,18,13],[23,18,21],[0,5,15],[16,3,20],[11,12,18],[0,12,9],[8,29,23],[8,12,4],[31,19,25],[10,26,16],[20,31,24],[9,28,27],[11,18,14],[27,21,0],[0,4,15],[15,10,27],[28,14,26],[16,25,5],[25,8,3],[26,12,24],[6,16,4],[7,18,27],[18,29,27],[26,22,13],[0,3,28],[20,4,21],[21,1,23],[21,5,12],[12,25,19],[24,9,5],[28,21,15],[12,29,7],[15,2,28],[20,2,13],[15,16,5],[11,0,8],[11,2,28],[11,19,20],[7,12,10],[26,19,31],[11,14,27],[1,31,15],[17,6,11],[12,10,28],[5,24,20],[22,19,24],[20,23,5],[2,8,9],[0,8,7],[8,3,21],[8,29,19],[20,6,15],[29,22,9],[31,7,22],[5,16,18],[1,31,28],[16,31,23],[30,27,10],[21,22,18],[3,8,12],[24,22,9],[17,30,19],[20,28,18],[14,2,17],[28,18,8],[14,27,31],[30,2,10],[12,0,6],[18,23,10],[21,12,13],[21,4,12],[13,5,28],[10,14,2],[26,8,27],[7,27,0],[23,7,4],[1,22,18],[31,23,13],[13,12,11],[27,17,10],[25,4,3],[19,15,12],[7,8,17],[26,11,27],[28,23,1],[12,30,26],[30,28,31],[6,7,22],[25,16,7],[14,9,8],[20,14,28],[12,15,13],[17,21,3],[7,12,5],[28,14,31],[0,17,9],[28,0,1],[10,28,6],[26,25,30],[3,13,31],[0,21,29],[2,18,23],[26,28,19],[23,3,31],[10,23,8],[28,31,14],[28,26,15],[4,25,30],[2,11,25],[14,0,16],[4,1,8],[11,17,14],[21,7,3],[29,17,21],[10,29,8],[23,8,5],[4,1,9],[26,18,23],[20,15,29],[17,16,12],[7,28,26],[1,14,31],[25,14,16],[12,15,20],[9,7,25],[26,7,10],[26,29,14],[2,18,1],[25,3,12],[10,26,17],[9,6,17],[14,1,10],[3,8,20],[20,24,7],[10,28,11],[24,20,5],[10,5,12],[12,27,30],[19,11,27],[0,4,1],[26,16,24],[7,19,24],[18,12,4],[30,23,0],[15,20,8],[30,14,23],[9,11,23],[27,9,18],[24,17,4],[0,24,16],[3,9,13],[6,15,13]],[[17,15,3],[5,11,9],[16,29,28],[4,23,10],[28,1,3],[13,27,17],[2,30,17],[19,1,3],[30,16,18],[4,12,2],[11,27,8],[19,9,27],[17,4,27],[11,23,31],[28,9,10],[24,28,9],[15,19,16],[18,27,1],[20,0,19],[1,22,6],[31,22,0],[3,26,4],[29,0,8],[3,9,5],[30,24,10],[10,31,6],[21,11,10],[18,17,22],[0,4,15],[19,0,23],[1,26,17],[24,28,30],[13,30,16],[1,27,0],[24,21,30],[5,20,31],[18,15,23],[20,19,16],[4,7,30],[3,22,6],[28,11,10],[7,22,30],[24,30,17],[6,12,25],[28,19,24],[27,22,31],[12,20,19],[23,9,30],[15,13,26],[24,6,2],[25,21,1],[15,26,28],[13,16,31],[10,24,23],[13,16,12],[23,16,27],[19,17,11],[1,30,31],[21,12,5],[22,3,10],[13,27,4],[22,10,31],[9,25,19],[21,6,18],[13,23,1],[21,11,28],[4,1,22],[7,9,16],[29,0,17],[8,1,13],[23,10,20],[0,13,23],[28,23,6],[23,31,2],[20,3,13],[29,14,22],[31,15,5],[20,19,5],[24,0,4],[9,0,12],[1,29,30],[28,0,25],[3,0,30],[23,9,1],[22,0,23],[1,24,10],[22,14,24],[23,2,19],[10,30,20],[26,11,30],[19,31,14],[5,14,28],[0,2,10],[21,15,16],[8,5,0],[11,22,4],[9,28,8],[29,25,28],[22,20,10],[3,26,23],[17,18,2],[4,17,12],[23,30,9],[7,12,19],[29,3,9],[4,10,16],[23,18,14],[20,30,2],[20,25,31],[1,30,13],[1,5,14],[4,20,31],[23,14,5],[0,21,19],[10,31,27],[27,8,31],[11,29,6],[26,13,17],[5,10,31],[10,11,1],[1,27,21],[25,5,21],[14,31,28],[17,29,26],[8,3,5],[24,9,0],[6,28,20],[27,12,9],[2,30,17],[17,28,0],[25,20,0],[31,0,22],[0,7,28],[15,3,17],[24,21,15],[30,27,2],[20,16,10],[19,7,29],[15,7,18],[9,31,12],[5,20,31],[7,3,10],[12,0,24],[21,27,14],[15,21,31],[16,11,26],[27,1,10],[9,19,4],[30,28,13],[13,11,23],[17,2,26],[30,24,20],[9,16,12],[14,27,7],[7,0,25],[14,26,2],[5,13,6],[5,6,19],[30,22,31],[19,10,24],[0,16,14],[23,12,15],[13,1,3],[22,10,3],[21,6,19],[31,5,8],[1,3,14],[25,17,26],[17,5,18],[3,8,6],[24,11,23],[5,17,19],[30,29,27],[10,23,28],[4,3,1],[30,5,9],[31,22,5],[9,5,24],[3,17,1],[22,12,20],[25,13,4],[2,26,24],[16,11,23],[1,22,27],[16,9,7],[30,26,7],[25,1,19],[4,7,22],[11,30,4],[17,27,30],[24,17,18],[8,16,15],[10,30,0],[8,0,29],[14,21,9],[31,5,22],[2,3,17],[29,5,16],[5,4,27],[15,12,28],[2,14,12],[10,13,30],[23,3,11],[30,12,22],[18,12,27],[23,28,8],[29,11,5],[14,11,15],[17,18,20],[26,22,6],[24,20,26],[28,0,24],[10,4,20],[18,21,8],[2,0,11],[25,9,29],[7,6,10],[24,28,7],[17,16,27],[6,11,7],[4,10,13],[18,9,25],[3,31,28],[21,17,4],[30,1,6],[12,23,15],[10,16,8],[24,25,19],[17,13,11],[9,17,21],[12,29,19],[8,13,18],[9,27,14],[29,28,19],[9,18,29],[12,0,22],[27,7,25],[24,21,9],[17,10,30],[12,9,29],[23,19,8],[18,9,1],[7,31,18],[6,11,12],[31,17,22],[20,22,10],[2,31,16],[10,22,12],[24,7,29],[2,27,23],[24,22,16],[3,5,12],[19,31,27],[15,5,16],[3,6,12],[20,5,3]],[[21,2,14],[1,16,29],[20,15,30],[9,30,3],[31,3,16],[16,20,8],[3,13,15],[2,4,26],[7,8,27],[13,23,31],[7,11,21],[17,29,3],[25,31,30],[16,5,31],[11,21,22],[28,8,6],[17,10,20],[12,30,16],[11,23,8],[29,4,1],[13,11,7],[25,26,27],[29,17,21],[3,30,16],[1,30,14],[7,2,17],[30,8,20],[28,19,23],[22,3,18],[18,17,0],[5,31,0],[30,16,5],[29,25,17],[22,23,13],[13,6,4],[26,19,12],[5,13,25],[19,29,26],[2,19,26],[22,20,14],[9,7,1],[27,3,12],[16,7,30],[14,15,11],[0,13,26],[14,24,15],[11,23,28],[31,26,7],[25,21,16],[3,9,22],[20,15,5],[0,21,15],[25,3,7],[19,18,20],[22,16,27],[29,16,11],[3,7,24],[0,17,18],[26,29,24],[16,3,15],[23,7,30],[19,13,12],[28,26,4],[2,5,17],[18,27,16],[11,30,17],[26,23,10],[9,26,3],[16,29,9],[27,4,21],[26,27,0],[16,0,13],[10,30,9],[7,11,18],[18,10,12],[14,4,22],[25,17,9],[8,28,7],[27,16,29],[18,19,9],[11,23,8],[2,7,3],[30,14,2],[27,25,29],[9,15,21],[6,27,24],[20,28,22],[7,4,11],[22,11,1],[4,30,11],[4,9,3],[27,0,15],[0,22,14],[6,0,14],[23,14,8],[16,20,18],[25,29,2],[20,3,21],[26,21,25],[9,1,15],[11,2,9],[3,15,25],[3,27,9],[25,8,19],[30,11,21],[10,12,24],[14,20,24],[13,11,12],[29,28,25],[13,10,22],[29,7,4],[28,17,24],[9,28,7],[12,16,24],[17,30,3],[29,30,24],[11,31,25],[29,27,3],[25,21,30],[2,27,31],[7,30,2],[22,9,23],[12,4,29],[7,0,13],[8,22,29],[0,4,8],[22,10,9],[29,20,9],[16,24,12],[1,3,12],[29,6,1],[26,8,0],[2,23,9],[7,25,31],[21,27,18],[23,21,0],[13,6,18],[22,6,11],[10,31,21],[25,15,19],[2,4,27],[9,22,31],[2,13,17],[19,4,29],[30,9,15],[22,5,4],[27,6,24],[8,12,28],[13,4,11],[16,8,10],[29,7,10],[20,18,3],[19,0,8],[20,13,21],[27,21,14],[13,6,23],[14,9,30],[23,15,8],[27,11,12],[12,20,29],[12,8,2],[13,24,31],[21,17,16],[23,13,5],[24,4,5],[12,30,25],[12,1,18],[25,20,0],[7,18,23],[20,21,22],[20,5,14],[14,10,27],[19,12,17],[3,17,10],[24,8,15],[17,25,9],[23,30,27],[24,6,13],[1,3,11],[15,21,30],[14,15,6],[21,19,18],[17,23,21],[19,4,1],[1,28,24],[16,20,12],[29,31,22],[26,15,25],[7,5,14],[20,17,25],[22,0,6],[15,9,2],[12,26,0],[29,15,30],[4,21,14],[1,2,31],[0,6,8],[28,24,12],[22,14,30],[24,29,7],[11,19,16],[18,16,30],[21,9,4],[21,6,19],[19,18,16],[25,1,23],[9,12,16],[4,9,0],[12,31,0],[10,30,31],[31,10,21],[11,19,23],[29,11,23],[24,28,4],[7,13,16],[6,11,21],[24,8,21],[12,4,6],[12,20,26],[19,0,16],[1,18,19],[10,29,23],[25,24,3],[7,31,15],[14,16,31],[3,14,17],[13,5,30],[29,10,7],[28,5,17],[16,1,26],[31,13,10],[16,4,14],[27,31,17],[13,30,21],[8,6,23],[13,22,2],[5,25,16],[23,16,5],[19,9,28],[11,27,31],[31,4,10],[3,29,12],[17,27,12],[21,4,29],[2,10,4],[1,18,14],[10,22,15],[6,23,27],[30,19,20],[26,8,22],[29,26,2],[12,25,23],[21,8,25],[7,1,30],[24,6,14],[14,19,21]],[[30,6,18],[25,1,22],[20,14,15],[17,27,5],[28,20,29],[11,27,28],[18,22,11],[2,22,6],[1,30,22],[31,3,29],[16,31,24],[16,6,7],[4,19,17],[7,18,5],[23,10,2],[1,23,21],[22,15,6],[4,0,11],[24,21,15],[20,14,22],[0,4,6],[20,12,3],[4,24,3],[2,18,13],[3,24,12],[28,8,1],[14,5,30],[24,3,25],[31,17,28],[31,13,17],[29,3,24],[29,13,28],[7,23,26],[0,4,29],[7,8,25],[4,7,19],[13,25,20],[21,25,6],[13,7,1],[11,6,28],[24,1,14],[13,6,3],[16,28,19],[26,22,13],[0,18,16],[21,14,26],[14,22,17],[2,26,22],[1,0,24],[18,20,11],[10,21,31],[15,5,2],[13,20,23],[5,6,18],[22,26,10],[25,19,31],[27,6,18],[9,1,6],[26,13,11],[10,25,4],[23,26,2],[19,18,23],[0,28,18],[13,5,26],[26,0,5],[4,10,31],[10,8,20],[29,18,13],[22,23,9],[26,0,30],[18,14,21],[13,27,12],[1,6,12],[30,2,14],[28,17,8],[12,20,24],[27,11,0],[1,17,21],[2,3,4],[17,27,2],[21,17,30],[7,12,19],[24,5,17],[23,14,17],[20,31,19],[16,28,21],[9,3,18],[9,16,13],[19,8,10],[6,4,5],[18,20,5],[29,16,30],[17,8,24],[2,17,28],[16,14,3],[31,19,2],[12,5,22],[27,28,6],[6,31,22],[26,13,12],[14,6,17],[23,16,10],[28,4,16],[19,8,16],[27,23,8],[16,28,12],[24,20,0],[5,7,8],[22,15,14],[5,17,6],[27,16,13],[9,19,31],[27,10,7],[22,28,23],[29,1,7],[4,12,28],[0,29,1],[26,17,27],[9,26,8],[15,30,21],[15,6,1],[31,1,27],[6,31,2],[18,1,7],[27,20,9],[15,0,6],[19,5,24],[25,2,22],[17,15,28],[8,27,15],[10,3,16],[0,2,31],[1,22,28],[19,20,3],[1,28,9],[8,19,10],[28,31,21],[26,9,29],[23,11,29],[3,19,2],[15,7,14],[7,29,27],[27,11,25],[13,25,5],[23,22,28],[10,15,23],[15,19,18],[7,6,28],[6,18,21],[28,26,31],[28,8,26],[22,24,1],[27,11,25],[8,29,24],[28,16,13],[5,14,28],[2,23,9],[20,4,21],[21,24,17],[9,22,31],[14,8,29],[3,12,27],[5,11,10],[17,29,20],[12,18,29],[0,11,4],[7,5,17],[24,2,4],[10,9,2],[20,1,19],[31,12,6],[2,8,13],[10,5,12],[7,13,0],[9,29,6],[20,28,16],[7,29,25],[28,20,19],[26,6,7],[15,9,11],[8,7,21],[2,23,31],[5,13,6],[30,5,25],[23,28,3],[9,11,6],[8,14,24],[18,17,10],[4,15,19],[11,13,15],[6,3,31],[23,15,12],[8,31,5],[15,16,20],[1,9,28],[17,7,1],[24,12,20],[18,2,15],[9,17,4],[14,10,31],[27,15,21],[4,30,20],[26,22,28],[21,7,12],[0,11,20],[24,30,5],[31,23,4],[31,8,20],[19,21,9],[18,14,2],[25,23,9],[10,7,28],[22,24,7],[8,29,15],[28,5,17],[22,16,12],[5,1,14],[21,9,24],[8,17,11],[27,29,18],[8,29,6],[25,24,29],[26,12,3],[17,11,4],[11,10,19],[18,21,17],[27,8,26],[0,4,20],[9,4,1],[13,3,19],[31,13,20],[26,25,30],[10,31,0],[20,25,12],[17,8,25],[20,7,10],[10,14,8],[31,0,19],[12,30,10],[0,10,17],[28,30,4],[3,13,9],[15,30,21],[8,14,13],[15,24,10],[13,28,10],[8,6,2],[26,31,20],[29,9,25],[19,25,14],[15,23,5],[21,5,27],[3,25,23],[10,12,16],[20,21,19],[6,8,12]],[[24,29,27],[14,25,18],[10,6,29],[24,11,29],[25,12,17],[12,28,15],[1,28,31],[31,8,29],[20,29,0],[15,31,8],[13,8,30],[11,27,5],[18,0,24],[18,9,0],[20,7,3],[0,2,19],[2,5,30],[5,14,4],[1,30,7],[27,1,29],[6,7,24],[24,21,1],[10,0,17],[22,8,15],[2,12,26],[5,10,3],[13,4,22],[6,16,23],[19,13,16],[18,11,10],[30,28,0],[25,28,23],[26,25,8],[18,24,0],[6,30,13],[20,16,15],[21,19,10],[31,14,17],[28,29,12],[23,9,11],[20,3,29],[27,15,13],[28,12,29],[14,6,4],[12,0,22],[24,7,11],[18,16,8],[28,0,22],[4,12,29],[4,22,21],[14,20,8],[17,29,27],[15,5,2],[24,27,1],[6,11,16],[10,29,2],[15,6,0],[6,12,27],[22,21,12],[1,2,15],[0,21,30],[20,22,29],[11,1,6],[16,31,18],[8,28,17],[20,14,2],[18,21,23],[9,2,21],[10,24,27],[2,15,22],[15,8,13],[13,26,2],[18,21,4],[24,19,5],[15,14,10],[5,4,30],[23,0,17],[13,0,7],[19,4,1],[27,18,3],[21,0,24],[0,25,10],[31,10,23],[5,28,16],[1,23,11],[27,24,16],[6,9,20],[27,5,11],[13,14,15],[26,12,5],[22,18,26],[17,2,22],[21,22,16],[19,18,8],[29,18,4],[6,4,28],[9,28,2],[3,21,15],[11,23,31],[19,9,29],[16,28,25],[5,0,13],[24,13,27],[1,13,19],[18,1,29],[27,21,23],[11,4,31],[21,3,0],[23,8,21],[4,8,13],[7,13,23],[3,21,30],[21,13,9],[9,12,18],[10,21,22],[23,5,18],[1,27,25],[24,27,26],[0,13,28],[8,22,10],[31,0,17],[27,0,2],[20,18,31],[6,13,3],[7,2,13],[9,12,22],[12,26,9],[23,24,2],[22,20,2],[25,27,24],[5,9,26],[0,19,5],[28,2,14],[24,12,25],[2,31,30],[23,9,1],[14,3,11],[19,17,31],[9,31,6],[2,24,14],[8,22,4],[19,0,10],[16,3,29],[22,28,20],[28,9,7],[10,7,14],[23,6,5],[11,15,17],[6,12,7],[19,14,31],[25,1,8],[21,17,23],[7,10,23],[1,30,11],[18,6,10],[20,6,21],[16,22,8],[15,22,10],[26,21,12],[24,10,12],[21,2,25],[30,7,20],[30,24,0],[26,30,25],[22,21,14],[21,11,5],[17,8,7],[2,3,7],[8,21,18],[9,1,19],[6,28,25],[9,5,7],[4,21,8],[25,20,26],[29,4,17],[29,7,28],[1,15,0],[29,24,13],[29,15,8],[20,10,2],[24,16,30],[5,3,8],[12,30,14],[1,17,21],[1,27,11],[24,21,30],[15,13,22],[27,22,17],[9,30,31],[23,2,17],[8,20,1],[14,19,4],[13,29,4],[10,17,30],[11,26,6],[24,31,18],[0,16,22],[29,17,2],[15,4,8],[2,16,28],[17,5,2],[15,4,10],[8,9,6],[5,29,26],[29,18,4],[29,28,17],[18,25,8],[10,15,0],[8,30,0],[30,8,6],[3,14,20],[31,0,17],[13,27,3],[24,0,30],[19,22,0],[16,24,31],[20,26,0],[28,2,6],[4,13,29],[30,5,17],[3,27,19],[30,25,8],[24,6,21],[25,14,19],[29,14,8],[24,5,11],[24,30,26],[19,17,29],[1,27,28],[30,0,25],[5,14,26],[14,12,8],[15,11,18],[16,30,1],[25,20,5],[5,9,10],[2,27,7],[0,19,22],[29,25,24],[16,6,19],[29,30,9],[26,9,20],[16,19,7],[15,5,28],[22,27,28],[31,9,19],[9,4,26],[18,1,17],[26,11,5],[16,26,21],[17,19,14],[11,21,28],[7,0,12],[29,28,0],[20,31,17],[4,31,10]],[[24,31,27],[22,25,12],[15,20,30],[7,30,19],[27,25,16],[9,31,10],[15,6,25],[19,23,17],[6,1,20],[0,22,28],[30,24,13],[23,16,2],[0,8,10],[17,6,22],[11,14,16],[15,29,20],[3,22,0],[6,30,19],[27,24,28],[26,27,21],[18,9,17],[23,28,8],[27,19,7],[29,22,5],[20,19,15],[8,23,15],[27,31,6],[11,29,6],[6,23,9],[18,20,26],[8,16,18],[4,22,23],[15,8,3],[28,1,25],[12,14,28],[21,18,26],[29,27,11],[11,1,4],[28,18,26],[23,31,27],[1,14,0],[0,15,10],[30,25,24],[17,11,8],[20,3,17],[13,28,29],[0,14,17],[9,18,21],[12,30,29],[22,8,4],[6,19,24],[22,17,31],[28,23,7],[13,29,30],[16,8,14],[18,23,5],[8,15,5],[5,2,1],[10,0,18],[30,4,22],[27,25,18],[29,23,2],[11,12,21],[14,24,9],[29,12,25],[17,4,13],[21,12,10],[3,20,2],[27,9,8],[23,0,10],[14,0,10],[0,6,5],[1,7,8],[30,16,21],[14,0,20],[24,25,5],[16,3,24],[20,25,12],[21,8,16],[6,13,10],[10,16,31],[22,6,10],[0,23,13],[11,18,9],[9,8,1],[6,3,0],[27,17,12],[19,30,21],[8,1,26],[6,0,21],[16,25,22],[11,19,2],[27,11,0],[7,15,13],[27,20,5],[29,18,26],[29,16,14],[4,7,30],[4,18,16],[23,14,22],[20,5,12],[5,25,22],[16,24,25],[5,8,21],[29,17,16],[2,11,26],[13,11,27],[29,28,0],[3,22,21],[25,0,8],[20,21,18],[9,28,21],[24,14,4],[10,6,22],[13,22,12],[19,29,10],[4,8,26],[15,24,27],[28,3,27],[0,29,30],[11,13,20],[27,20,2],[4,18,8],[30,29,21],[31,8,14],[11,4,25],[0,10,26],[3,12,13],[31,1,11],[28,0,4],[23,28,12],[12,27,19],[19,5,12],[27,14,4],[14,22,16],[19,24,23],[4,19,15],[16,8,6],[27,6,5],[26,31,11],[4,22,15],[21,0,2],[23,15,30],[26,24,30],[2,25,21],[21,7,4],[23,20,0],[21,18,29],[5,19,3],[16,24,25],[26,4,31],[23,13,6],[24,1,18],[6,9,27],[23,14,13],[27,31,20],[2,22,21],[16,19,20],[8,19,4],[14,26,15],[31,27,30],[18,31,16],[24,8,27],[7,29,24],[6,28,8],[22,29,17],[23,26,7],[16,24,29],[0,12,19],[22,31,12],[12,3,18],[6,12,26],[12,17,10],[14,3,22],[17,29,3],[16,18,19],[12,16,8],[21,8,26],[0,16,15],[28,14,31],[2,11,27],[10,19,21],[8,21,0],[3,31,27],[0,31,23],[14,11,7],[1,14,18],[29,21,31],[0,28,30],[19,8,0],[5,19,3],[25,24,0],[20,19,4],[9,19,24],[21,26,14],[11,15,28],[8,24,3],[19,26,4],[23,15,26],[16,27,19],[21,0,16],[15,31,5],[4,11,15],[26,5,16],[1,9,13],[30,16,21],[27,6,17],[2,15,22],[5,2,18],[4,2,16],[19,21,10],[27,22,8],[7,20,3],[18,5,14],[2,17,19],[29,13,31],[14,21,15],[11,7,24],[21,10,24],[31,10,30],[2,8,4],[12,0,23],[19,24,1],[13,9,8],[2,31,11],[8,0,22],[28,11,2],[0,2,15],[17,5,13],[21,12,5],[17,6,13],[9,31,16],[9,8,18],[9,15,19],[25,26,5],[31,10,9],[18,26,1],[12,0,1],[15,3,27],[26,23,13],[0,25,21],[13,23,28],[18,21,24],[17,2,6],[1,13,7],[2,9,17],[16,28,12],[14,23,10],[4,25,31],[5,29,27],[8,5,6],[27,19,5],[16,9,30],[29,23,11],[14,28,23],[10,22,13]],[[14,23,13],[27,7,8],[29,20,22],[9,0,16],[24,16,9],[11,0,10],[8,21,7],[20,2,4],[19,22,31],[12,18,6],[12,13,27],[0,16,24],[13,0,29],[1,30,18],[1,4,6],[12,15,16],[14,9,5],[25,28,2],[15,12,29],[20,28,16],[7,29,3],[29,22,3],[14,28,20],[9,1,31],[30,28,18],[1,6,15],[5,9,12],[25,24,8],[14,7,4],[0,16,6],[2,9,22],[23,26,31],[29,5,26],[17,0,24],[8,31,4],[31,6,9],[29,6,13],[7,27,15],[6,15,30],[12,19,11],[10,23,21],[26,15,29],[10,20,9],[11,0,30],[31,0,4],[15,0,27],[31,27,17],[12,3,1],[30,13,23],[31,2,23],[23,5,14],[1,9,16],[5,22,17],[0,22,6],[11,25,8],[28,18,0],[26,13,19],[26,17,1],[7,3,23],[28,17,20],[21,2,7],[30,14,12],[10,0,30],[3,23,13],[4,3,31],[29,12,16],[19,11,6],[28,16,1],[24,9,23],[7,10,2],[0,11,8],[24,3,21],[25,30,11],[19,20,13],[24,0,8],[11,21,16],[5,19,0],[22,9,29],[17,2,23],[5,25,15],[22,20,14],[15,10,14],[31,25,13],[26,12,31],[30,27,8],[10,27,7],[9,2,30],[29,14,25],[17,21,0],[24,11,17],[5,18,17],[10,11,2],[30,7,6],[31,27,0],[9,16,28],[5,11,0],[0,26,5],[15,13,1],[12,2,7],[26,14,22],[27,0,10],[13,14,4],[18,24,17],[4,22,26],[4,25,20],[4,28,3],[3,27,26],[31,21,0],[26,8,24],[17,28,10],[13,5,1],[1,13,7],[25,22,24],[19,28,20],[26,12,3],[7,1,3],[19,15,7],[30,5,8],[3,14,30],[19,10,21],[26,23,15],[20,13,23],[26,4,15],[29,28,22],[6,31,9],[9,6,14],[17,9,16],[7,12,4],[20,11,19],[1,6,13],[4,25,23],[14,15,3],[0,12,10],[29,22,24],[21,5,7],[0,1,11],[1,5,7],[19,0,4],[29,3,21],[2,24,16],[25,0,10],[24,8,0],[7,0,11],[23,13,1],[26,8,25],[29,12,4],[15,19,4],[21,15,0],[19,14,8],[27,19,11],[0,15,25],[7,28,3],[22,0,21],[0,18,5],[19,31,18],[14,29,4],[26,18,15],[8,23,18],[11,29,20],[28,0,29],[12,17,0],[25,29,15],[6,1,28],[23,28,20],[10,23,24],[17,4,13],[0,3,31],[17,15,6],[12,22,29],[29,13,9],[29,2,7],[11,15,0],[1,31,8],[21,15,20],[15,25,18],[15,2,17],[10,30,31],[13,8,12],[13,14,9],[21,16,17],[16,30,22],[2,31,29],[5,14,26],[0,2,5],[0,6,20],[7,1,29],[0,6,28],[23,10,25],[22,15,3],[3,18,6],[3,18,19],[6,23,8],[30,16,5],[0,24,1],[13,7,10],[12,19,18],[21,1,23],[29,12,11],[4,29,27],[14,6,26],[29,19,26],[16,6,23],[22,23,10],[11,1,25],[28,15,20],[14,3,0],[11,4,21],[23,25,9],[30,10,0],[17,30,4],[15,4,25],[11,5,0],[11,10,14],[31,12,25],[13,18,12],[13,29,24],[28,2,19],[30,22,18],[14,23,10],[28,2,8],[19,31,12],[15,30,2],[13,23,8],[2,6,17],[3,11,19],[24,9,12],[18,13,11],[18,30,3],[26,13,1],[13,17,11],[25,10,21],[5,4,17],[1,18,13],[25,19,12],[19,23,0],[19,8,1],[30,17,15],[7,3,24],[11,12,1],[12,5,9],[2,19,1],[21,10,2],[30,6,7],[22,26,27],[16,8,12],[5,3,12],[17,29,26],[10,17,14],[0,17,18],[13,1,19],[19,16,13],[30,25,0],[25,10,12],[20,17,27],[4,30,19],[8,22,13]],[[7,20,11],[8,18,26],[28,18,0],[4,24,23],[19,6,11],[23,6,30],[2,29,31],[19,29,22],[29,23,14],[18,4,2],[15,7,1],[21,19,28],[11,23,13],[17,28,21],[23,15,12],[18,20,13],[9,17,5],[29,22,17],[30,17,15],[4,16,17],[16,18,14],[9,23,16],[21,27,28],[31,22,20],[23,25,12],[0,3,10],[7,28,17],[28,19,11],[11,18,17],[12,21,19],[16,9,3],[1,22,27],[25,27,20],[27,28,25],[22,21,2],[26,2,19],[8,7,6],[27,21,31],[27,4,13],[15,2,23],[19,11,17],[29,22,15],[23,17,11],[13,18,26],[3,24,25],[26,22,9],[2,27,22],[23,31,8],[15,13,28],[11,13,26],[11,8,0],[1,22,9],[24,20,13],[6,28,24],[5,23,11],[20,16,21],[25,11,23],[24,11,21],[24,25,6],[6,15,5],[13,3,16],[25,28,7],[29,2,1],[11,6,29],[3,27,12],[20,26,17],[8,28,7],[15,7,29],[10,20,5],[25,30,23],[17,12,2],[3,0,1],[15,19,11],[11,0,9],[4,15,7],[20,11,29],[6,11,24],[0,13,9],[4,16,2],[17,12,31],[25,18,29],[1,6,12],[14,3,2],[22,5,16],[27,28,25],[18,0,28],[18,17,26],[19,23,5],[30,17,9],[26,7,22],[26,23,13],[27,24,15],[15,28,10],[19,2,26],[7,11,20],[10,30,14],[8,0,17],[7,10,0],[11,28,18],[2,28,6],[25,0,29],[27,26,0],[11,23,20],[21,24,23],[23,28,7],[11,9,29],[9,7,2],[19,26,4],[14,12,21],[19,2,22],[17,13,16],[29,14,17],[9,3,29],[28,11,19],[20,25,26],[7,11,2],[24,1,22],[9,6,16],[6,8,7],[24,11,0],[15,31,25],[4,23,28],[19,17,14],[29,12,15],[19,1,10],[29,31,7],[1,7,9],[5,6,0],[30,20,16],[0,16,9],[29,1,11],[4,13,19],[25,6,4],[24,19,31],[9,13,2],[12,31,24],[24,11,26],[25,18,7],[19,5,31],[23,5,22],[23,31,5],[13,3,14],[22,3,20],[27,10,11],[31,9,11],[5,13,25],[24,18,20],[27,28,12],[18,25,1],[24,23,11],[7,11,18],[18,10,9],[1,17,4],[4,6,20],[17,7,3],[2,1,20],[5,17,20],[25,19,23],[3,21,24],[9,17,31],[29,8,20],[19,18,22],[13,1,11],[28,19,29],[2,14,11],[23,13,12],[19,28,5],[19,27,30],[6,2,5],[11,27,18],[9,30,8],[19,12,16],[13,10,29],[24,21,12],[22,1,8],[24,1,21],[31,28,3],[2,15,12],[22,25,15],[17,13,8],[18,26,2],[7,12,11],[26,0,20],[21,16,8],[30,29,11],[14,5,24],[18,10,28],[14,30,2],[1,20,25],[18,8,16],[26,16,31],[5,11,14],[11,19,30],[3,16,31],[18,25,22],[18,8,24],[18,17,10],[31,2,24],[26,2,3],[8,29,12],[7,1,2],[10,6,21],[14,22,29],[4,24,23],[26,27,16],[12,11,18],[22,11,13],[6,15,9],[24,16,9],[23,29,5],[23,0,11],[21,23,2],[20,13,25],[10,1,8],[27,5,3],[15,2,26],[24,8,11],[19,31,23],[29,4,11],[12,27,20],[0,9,21],[11,13,15],[1,25,24],[19,7,4],[14,10,4],[19,7,20],[25,12,29],[12,13,6],[5,18,21],[21,31,14],[3,2,13],[6,2,15],[12,27,3],[19,4,3],[3,10,7],[27,11,14],[6,20,22],[6,12,25],[30,4,10],[10,14,4],[1,21,13],[24,20,0],[21,2,3],[4,25,20],[20,5,11],[28,9,29],[13,28,8],[27,4,3],[22,31,9],[18,22,4],[26,17,25],[14,25,3],[8,0,12],[12,29,26],[7,23,18],[18,31,16]],[[0,26,18],[13,29,31],[0,18,29],[27,29,24],[15,27,17],[27,10,3],[26,18,25],[17,21,20],[26,1,12],[3,25,0],[18,17,9],[20,26,16],[20,27,17],[10,24,12],[28,8,20],[10,31,28],[27,11,29],[31,6,24],[19,20,3],[26,5,19],[11,27,21],[19,1,27],[13,3,30],[30,6,23],[3,2,31],[27,20,23],[8,27,15],[23,6,31],[10,29,23],[5,7,4],[21,19,22],[27,3,28],[8,7,5],[12,30,16],[1,26,19],[22,2,17],[3,21,26],[18,10,7],[30,28,31],[5,23,14],[4,30,5],[12,4,10],[11,21,19],[24,22,12],[10,4,16],[0,23,4],[5,18,9],[22,25,21],[8,12,21],[14,20,6],[18,10,1],[7,18,9],[7,26,12],[29,21,22],[3,0,15],[10,17,1],[20,4,10],[25,28,13],[17,18,19],[12,14,0],[2,8,29],[10,1,20],[4,24,22],[20,8,30],[18,11,13],[4,9,17],[27,23,0],[21,24,6],[28,24,9],[14,2,18],[29,2,23],[12,17,3],[25,6,12],[18,25,2],[15,23,7],[20,2,21],[13,25,4],[6,11,21],[17,3,5],[16,23,21],[26,18,14],[8,1,30],[26,6,20],[6,19,4],[0,17,16],[23,6,18],[29,6,19],[26,0,5],[28,22,3],[3,29,30],[16,17,31],[28,30,3],[27,14,16],[30,7,10],[7,31,19],[1,30,0],[9,20,30],[2,6,31],[1,9,2],[14,18,29],[26,13,14],[31,30,6],[1,31,30],[5,12,30],[5,26,31],[27,9,22],[16,6,8],[5,1,9],[18,6,28],[31,1,22],[4,24,8],[10,17,14],[24,10,8],[22,26,5],[16,21,20],[28,9,24],[3,13,20],[11,10,16],[26,19,0],[21,5,13],[21,30,3],[19,28,16],[7,18,11],[23,24,1],[7,2,19],[2,21,8],[19,24,23],[2,5,28],[3,17,20],[17,27,8],[2,26,16],[19,25,16],[13,29,31],[10,22,28],[25,20,6],[9,2,13],[30,23,4],[5,25,17],[3,5,1],[29,17,22],[12,16,1],[14,6,28],[23,11,22],[24,30,14],[5,7,2],[16,21,1],[7,29,11],[29,0,23],[24,23,4],[12,7,8],[16,14,25],[12,23,0],[14,16,6],[21,24,6],[19,23,17],[25,2,14],[20,29,18],[25,8,17],[30,3,20],[3,24,17],[23,16,12],[24,26,6],[5,15,19],[25,1,5],[18,25,7],[21,0,16],[13,29,19],[31,7,28],[8,2,13],[13,6,4],[29,7,21],[15,0,6],[15,10,18],[6,2,13],[14,16,22],[26,31,11],[16,22,5],[27,22,17],[25,20,26],[0,27,11],[12,20,0],[6,14,27],[9,28,13],[2,16,28],[28,10,4],[22,26,27],[28,26,29],[6,13,7],[23,0,28],[1,0,22],[18,31,25],[13,25,1],[19,8,10],[30,1,21],[26,31,12],[24,18,4],[16,23,20],[26,10,11],[3,13,9],[19,22,4],[17,21,28],[12,27,13],[12,11,0],[31,16,25],[8,14,12],[17,3,18],[4,26,5],[14,10,4],[10,8,27],[23,14,26],[11,17,13],[23,0,17],[9,18,10],[10,15,24],[29,0,30],[7,12,27],[4,9,10],[22,3,1],[29,18,9],[28,9,30],[16,12,25],[26,24,17],[17,14,23],[24,0,14],[1,18,26],[3,25,11],[6,13,0],[13,31,15],[7,22,28],[12,21,11],[10,21,5],[18,15,7],[31,8,9],[28,29,8],[25,21,3],[11,2,10],[6,12,20],[31,18,20],[13,7,22],[8,1,30],[15,11,19],[12,19,20],[7,31,12],[25,31,28],[16,0,30],[25,18,6],[17,24,0],[21,14,24],[2,24,5],[27,11,28],[17,14,13],[27,8,21],[7,3,16],[17,1,21],[22,0,26],[23,5,19]],[[5,13,10],[16,20,17],[27,5,21],[29,25,26],[20,13,8],[12,14,9],[6,4,23],[8,20,18],[26,23,29],[7,5,13],[15,5,13],[26,6,15],[16,18,30],[30,7,10],[16,9,1],[1,14,31],[13,4,5],[12,21,8],[30,31,17],[7,9,12],[11,27,12],[20,25,9],[21,12,20],[14,21,26],[31,12,22],[29,26,15],[12,9,0],[14,28,4],[29,16,18],[1,25,9],[13,7,19],[0,1,27],[4,24,9],[18,23,19],[12,21,11],[15,20,19],[23,28,25],[21,1,22],[6,23,5],[23,2,27],[17,25,2],[22,16,26],[30,14,18],[30,16,11],[10,2,11],[2,20,22],[23,17,22],[16,9,6],[25,12,26],[8,12,20],[26,8,10],[1,7,19],[11,9,15],[22,16,2],[16,7,10],[3,26,15],[30,25,1],[1,21,26],[11,9,2],[11,30,6],[27,16,13],[14,24,27],[30,8,13],[25,1,0],[10,26,5],[28,20,4],[1,8,23],[15,8,31],[1,31,20],[5,9,12],[9,21,2],[3,11,18],[1,29,14],[29,12,30],[24,28,18],[9,13,19],[29,31,25],[1,3,7],[25,17,29],[4,13,27],[12,1,13],[14,5,28],[25,13,12],[20,14,18],[9,16,20],[10,30,22],[21,30,3],[31,1,30],[28,29,4],[1,15,9],[15,8,19],[2,9,30],[9,10,16],[31,24,2],[17,1,19],[3,21,4],[15,3,28],[2,27,7],[9,18,4],[31,8,19],[2,23,10],[25,26,1],[16,18,23],[30,10,5],[18,20,29],[3,18,6],[10,24,14],[2,19,10],[4,5,19],[24,11,21],[27,1,10],[0,30,16],[1,15,7],[31,21,0],[22,20,10],[17,14,22],[8,9,28],[11,26,21],[2,6,24],[20,31,2],[27,12,14],[22,6,19],[28,27,22],[31,28,25],[9,11,13],[11,28,22],[13,11,18],[30,31,13],[15,27,20],[21,11,4],[22,12,26],[22,26,30],[30,13,3],[12,31,13],[27,30,4],[9,29,25],[22,10,29],[16,23,17],[16,31,29],[31,28,30],[31,26,0],[18,28,1],[19,10,17],[28,9,31],[1,4,17],[27,0,8],[17,0,4],[14,16,9],[2,14,16],[17,23,14],[24,25,3],[15,18,29],[3,26,20],[3,15,12],[6,30,0],[11,23,7],[30,10,9],[4,30,26],[15,12,13],[27,3,15],[31,4,3],[5,27,22],[25,10,20],[28,3,26],[26,10,7],[16,7,15],[31,12,17],[17,7,29],[7,4,5],[20,16,27],[18,28,1],[13,3,11],[13,25,10],[12,25,6],[14,31,13],[29,13,31],[30,18,20],[11,31,12],[12,17,16],[28,19,9],[27,20,26],[1,24,21],[28,24,19],[2,31,23],[30,21,25],[9,12,19],[21,10,16],[29,8,24],[20,17,16],[14,23,19],[11,27,7],[2,0,7],[27,29,3],[29,6,24],[20,23,5],[0,9,6],[24,10,22],[2,21,20],[15,0,29],[9,11,8],[11,18,16],[0,10,18],[9,13,16],[16,17,27],[30,13,31],[24,1,16],[11,8,19],[29,23,26],[9,25,15],[16,3,1],[9,0,5],[21,19,27],[22,7,8],[3,24,17],[21,25,27],[29,11,20],[0,16,31],[23,27,0],[3,6,1],[27,14,3],[4,22,26],[5,12,16],[16,12,7],[17,10,31],[29,26,15],[19,21,7],[21,28,15],[12,30,1],[26,5,9],[4,1,31],[21,2,12],[11,19,29],[8,27,12],[19,26,17],[13,26,11],[13,21,24],[12,30,17],[27,13,10],[25,9,26],[8,23,30],[2,10,13],[6,2,8],[31,18,20],[19,5,9],[10,19,14],[24,18,11],[8,11,24],[16,10,24],[16,18,21],[17,25,9],[25,9,28],[8,2,31],[9,0,24],[13,28,18],[21,23,10],[19,30,17]],[[7,24,5],[22,14,30],[23,25,30],[11,27,9],[0,25,27],[16,17,14],[7,16,23],[4,18,7],[9,30,12],[23,5,6],[15,16,17],[31,8,14],[17,4,25],[29,0,4],[22,7,29],[1,17,14],[12,7,15],[18,19,17],[24,28,8],[23,0,30],[21,24,4],[10,21,14],[14,0,26],[26,14,8],[10,19,8],[11,23,22],[27,16,3],[9,3,21],[4,22,9],[2,18,25],[29,1,25],[6,22,30],[18,15,28],[29,12,16],[12,13,9],[19,16,9],[21,26,11],[1,4,2],[25,8,12],[30,14,31],[6,15,19],[17,12,20],[17,18,6],[5,6,2],[8,11,1],[29,27,4],[29,21,23],[9,19,20],[0,27,31],[25,18,7],[4,6,3],[8,14,17],[10,14,26],[2,7,21],[9,16,30],[2,24,5],[4,15,0],[30,26,19],[26,18,5],[20,27,31],[5,6,4],[13,18,23],[8,25,23],[13,10,22],[31,9,4],[26,9,30],[21,11,27],[3,12,0],[26,0,5],[13,11,29],[19,30,2],[17,30,26],[25,13,29],[23,7,28],[5,15,10],[15,27,7],[4,23,31],[16,28,21],[24,25,2],[11,27,15],[5,6,2],[13,1,31],[11,5,19],[10,18,21],[4,9,17],[29,4,16],[16,10,22],[9,26,21],[4,21,8],[27,6,20],[20,9,17],[21,9,24],[5,17,10],[8,19,17],[19,8,1],[7,24,11],[19,15,12],[28,3,16],[15,11,6],[3,11,6],[1,31,18],[20,11,19],[22,4,21],[10,7,25],[21,28,23],[14,7,2],[4,24,14],[17,22,13],[10,11,13],[2,29,28],[16,19,26],[31,1,14],[4,24,13],[17,7,3],[24,17,27],[15,2,28],[17,8,29],[18,12,0],[24,21,12],[20,27,19],[18,24,22],[28,6,20],[9,21,0],[18,26,5],[12,13,30],[20,10,9],[5,27,11],[14,25,19],[5,28,13],[10,16,0],[3,20,4],[5,25,1],[11,31,10],[21,26,25],[14,3,25],[26,6,4],[21,23,9],[8,17,0],[31,23,11],[26,15,11],[0,5,31],[12,5,21],[31,21,2],[12,0,25],[1,13,12],[7,20,3],[3,8,22],[10,5,9],[10,14,11],[10,30,19],[21,24,30],[31,8,7],[11,30,17],[1,24,27],[21,17,20],[28,30,18],[13,8,11],[12,15,0],[11,16,20],[27,14,7],[1,26,29],[17,28,18],[4,22,3],[29,14,31],[28,1,30],[29,13,8],[20,15,24],[9,27,10],[14,13,2],[23,14,2],[2,18,12],[21,25,4],[7,0,27],[16,21,25],[10,15,27],[30,2,21],[26,13,11],[2,13,8],[0,2,12],[23,21,6],[11,22,9],[22,19,27],[3,21,22],[19,1,4],[12,29,15],[3,21,6],[28,27,15],[27,23,11],[0,13,17],[9,26,18],[13,29,31],[12,25,9],[10,30,9],[22,2,28],[9,5,28],[1,4,25],[21,6,19],[31,20,27],[15,0,16],[25,16,14],[22,6,17],[2,4,6],[20,26,15],[23,16,19],[30,21,23],[1,6,25],[4,13,14],[7,30,1],[17,25,24],[29,11,26],[31,14,2],[3,28,1],[6,20,12],[12,17,16],[28,19,12],[23,31,8],[27,29,5],[17,18,3],[9,24,21],[29,21,17],[8,3,28],[1,2,20],[9,16,28],[2,25,28],[17,12,5],[18,7,10],[21,30,3],[8,1,21],[1,29,20],[10,23,8],[29,0,24],[28,4,18],[9,1,16],[0,17,7],[0,30,28],[27,22,4],[12,10,7],[7,26,8],[14,25,17],[25,9,8],[17,22,4],[21,27,31],[25,7,1],[20,3,12],[5,6,19],[30,21,20],[31,8,25],[15,20,17],[5,17,19],[1,28,24],[19,6,4],[30,23,14],[10,16,9],[2,12,21],[25,27,2],[21,14,9]],[[11,8,22],[19,25,30],[16,0,25],[11,15,21],[5,12,2],[18,26,14],[13,0,21],[20,13,9],[29,20,18],[27,24,28],[0,30,29],[0,22,20],[12,21,0],[19,9,12],[28,22,21],[20,19,2],[27,13,17],[1,14,4],[28,29,12],[30,15,5],[2,3,1],[28,26,2],[26,28,6],[22,8,4],[5,29,25],[21,19,10],[25,21,13],[15,26,30],[7,29,27],[3,14,4],[22,26,11],[12,1,13],[12,6,19],[27,25,17],[20,16,2],[7,13,18],[5,15,30],[29,26,10],[4,11,23],[6,24,16],[0,2,6],[17,9,0],[2,26,5],[0,18,20],[10,5,28],[13,12,29],[11,18,23],[21,10,26],[30,5,26],[17,5,1],[27,21,19],[10,4,21],[25,15,6],[19,4,1],[14,23,30],[29,21,28],[19,26,20],[23,7,16],[30,27,2],[25,2,10],[3,10,12],[17,31,29],[30,12,14],[9,25,1],[25,18,14],[14,2,1],[16,9,22],[7,28,21],[25,24,28],[14,19,0],[8,17,15],[26,3,15],[19,4,23],[20,16,24],[16,18,13],[4,20,16],[19,11,7],[30,29,25],[1,3,25],[24,30,4],[21,25,18],[18,6,16],[6,17,29],[14,19,30],[9,16,7],[18,28,21],[12,16,4],[15,24,17],[28,17,7],[2,15,24],[2,15,24],[30,13,28],[7,14,8],[18,12,13],[18,11,2],[12,20,27],[26,10,14],[18,10,15],[8,11,0],[24,16,26],[7,24,27],[9,22,7],[3,20,30],[31,6,13],[18,31,3],[16,27,4],[8,31,1],[2,11,6],[4,30,7],[18,23,30],[0,1,23],[15,28,29],[14,15,3],[22,17,5],[4,2,18],[5,13,11],[26,1,9],[2,30,18],[9,15,21],[11,13,16],[3,8,22],[21,17,18],[17,7,26],[3,16,0],[10,12,19],[10,16,1],[11,5,7],[25,7,11],[3,30,26],[27,15,10],[23,20,10],[27,28,26],[28,14,29],[2,17,25],[0,11,26],[22,4,5],[19,16,25],[25,15,13],[6,5,3],[27,16,17],[3,4,10],[25,29,28],[27,1,10],[15,20,18],[6,22,20],[18,29,28],[0,13,3],[2,24,30],[26,10,7],[29,11,1],[10,26,13],[10,25,17],[9,0,23],[25,0,27],[28,6,5],[0,10,31],[15,24,13],[27,13,25],[15,20,13],[24,10,14],[22,29,28],[31,26,1],[15,18,27],[8,28,26],[19,28,29],[7,4,24],[16,10,23],[28,10,12],[7,13,12],[14,3,31],[9,14,30],[3,13,12],[24,12,7],[28,20,29],[3,17,30],[15,13,31],[10,30,12],[26,16,6],[26,29,23],[15,21,29],[2,1,30],[31,12,28],[16,15,27],[10,19,28],[14,19,2],[26,13,11],[10,20,15],[2,29,23],[19,22,15],[13,5,30],[5,3,28],[17,12,22],[24,6,18],[28,0,21],[27,25,10],[6,11,3],[20,0,7],[4,3,30],[9,6,22],[26,13,15],[27,8,2],[19,26,21],[1,26,17],[6,25,10],[31,2,28],[7,21,14],[17,20,18],[18,15,19],[18,1,29],[5,27,24],[19,30,12],[16,0,1],[7,17,27],[25,17,6],[29,9,12],[4,7,3],[10,2,30],[20,23,3],[25,17,21],[5,15,7],[1,12,20],[12,0,30],[12,10,22],[2,1,18],[24,26,17],[2,28,5],[21,3,15],[5,21,7],[2,14,25],[4,13,6],[20,25,2],[1,16,6],[26,3,15],[11,0,6],[0,6,27],[22,28,26],[12,0,30],[29,7,26],[22,21,5],[20,16,31],[21,15,13],[4,18,28],[9,29,11],[16,6,10],[13,26,9],[17,19,21],[23,9,7],[22,23,27],[4,16,24],[26,12,29],[1,26,8],[12,28,18],[1,12,22],[7,23,12],[28,20,23],[15,14,29]],[[6,8,26],[15,30,31],[22,13,18],[27,18,1],[28,20,27],[31,9,6],[30,16,22],[27,5,7],[18,0,28],[16,2,5],[15,31,4],[26,15,20],[1,28,11],[17,19,27],[27,28,30],[29,24,18],[10,29,22],[1,31,16],[25,7,28],[8,31,1],[6,20,19],[1,3,19],[22,3,4],[31,12,30],[23,13,15],[12,4,28],[14,6,15],[31,11,14],[17,8,3],[10,29,5],[3,17,18],[6,20,4],[11,5,25],[4,15,12],[1,7,19],[11,2,23],[23,6,7],[29,28,10],[3,16,2],[2,16,1],[23,1,30],[8,10,0],[20,7,16],[30,23,0],[10,0,30],[10,25,29],[28,9,8],[4,31,9],[23,1,24],[11,27,0],[9,29,27],[19,30,17],[2,16,0],[26,30,8],[31,29,17],[31,17,19],[23,21,1],[24,10,0],[6,16,2],[24,5,16],[21,25,23],[10,29,1],[31,28,16],[28,8,2],[5,18,26],[8,21,26],[18,6,31],[14,15,30],[13,30,7],[18,14,20],[23,12,4],[2,28,3],[27,9,0],[10,31,5],[23,6,28],[7,4,24],[21,3,5],[19,6,15],[25,9,2],[13,21,11],[22,21,4],[0,16,19],[19,2,21],[8,21,30],[24,5,8],[27,31,1],[2,21,30],[17,4,1],[17,22,3],[4,29,16],[0,5,13],[14,31,30],[17,10,8],[21,23,14],[14,7,3],[28,0,10],[23,6,3],[26,1,19],[29,28,1],[30,23,20],[13,21,28],[20,9,11],[0,13,20],[26,13,27],[2,21,4],[2,26,7],[7,27,5],[14,15,11],[14,7,16],[31,1,4],[25,18,13],[29,21,22],[5,16,31],[22,11,12],[16,2,22],[15,27,9],[4,15,7],[11,2,12],[15,17,24],[17,26,1],[16,22,1],[19,23,28],[23,6,25],[12,20,5],[20,15,27],[23,20,31],[7,2,24],[0,11,21],[18,31,16],[23,31,13],[7,16,25],[23,19,21],[30,2,13],[28,5,18],[14,2,12],[12,31,14],[30,22,1],[3,29,9],[24,8,15],[28,0,6],[30,18,1],[1,16,28],[8,5,7],[6,3,11],[15,8,23],[17,8,18],[21,4,22],[18,22,21],[8,0,3],[24,14,18],[4,18,26],[12,28,24],[7,13,27],[21,3,16],[28,7,12],[3,25,14],[7,5,12],[10,6,19],[22,29,16],[14,29,17],[3,31,5],[2,5,3],[17,31,18],[6,1,7],[6,28,9],[18,7,26],[31,15,11],[3,9,22],[15,14,10],[15,19,12],[22,26,9],[10,31,2],[17,18,10],[7,19,21],[31,15,0],[17,13,24],[15,10,28],[10,14,19],[12,0,26],[21,23,22],[30,4,10],[10,29,25],[10,5,8],[14,0,3],[11,19,25],[10,5,18],[18,3,7],[8,0,12],[27,9,19],[17,5,2],[2,23,27],[13,18,11],[27,23,11],[27,23,30],[30,31,22],[7,14,15],[4,19,17],[11,21,0],[6,21,0],[14,21,26],[16,28,21],[11,22,1],[6,26,18],[23,19,26],[7,23,0],[24,15,16],[11,13,17],[11,27,13],[3,27,5],[24,14,26],[9,23,15],[7,14,17],[4,20,9],[15,27,14],[7,21,25],[15,7,29],[20,3,7],[0,29,25],[24,3,8],[25,17,19],[16,12,13],[13,26,24],[17,28,22],[26,0,10],[20,7,10],[16,6,7],[12,14,19],[6,1,7],[6,21,1],[22,18,20],[24,14,5],[15,23,21],[13,23,21],[24,18,27],[23,13,21],[30,28,24],[12,21,9],[6,28,27],[4,30,24],[14,9,21],[18,8,29],[16,28,12],[1,8,3],[13,3,30],[19,6,16],[19,29,26],[19,30,9],[14,29,22],[16,8,21],[17,13,25],[13,27,28],[24,17,19],[16,8,19],[24,13,27],[14,25,28],[11,6,17]],[[12,21,0],[16,15,5],[27,2,26],[20,10,27],[0,8,10],[31,6,15],[23,0,27],[2,13,15],[22,20,7],[12,8,11],[20,16,3],[6,30,24],[13,19,30],[19,0,16],[4,20,13],[19,9,30],[22,15,10],[31,2,29],[15,6,24],[27,13,12],[3,0,13],[31,5,0],[2,4,9],[30,23,17],[0,4,27],[21,23,4],[6,31,3],[15,19,7],[27,30,9],[12,5,19],[27,7,9],[10,25,15],[5,22,4],[4,16,10],[31,14,19],[18,15,14],[14,5,16],[29,19,10],[10,2,5],[7,8,29],[14,10,22],[17,14,26],[26,1,29],[31,9,1],[19,22,13],[6,3,10],[17,6,26],[9,5,8],[30,4,20],[24,13,5],[4,22,14],[21,27,9],[15,9,8],[18,16,8],[24,2,15],[20,28,21],[27,8,24],[6,20,23],[19,9,16],[8,25,18],[6,3,10],[30,31,4],[17,15,22],[30,20,23],[23,28,18],[8,13,21],[1,7,15],[0,20,8],[19,26,10],[2,30,14],[1,24,14],[9,0,21],[0,2,25],[10,27,16],[13,4,10],[10,14,30],[28,8,1],[13,29,17],[16,17,30],[15,27,9],[7,12,26],[1,20,8],[26,4,30],[19,13,7],[15,12,28],[3,28,19],[28,30,24],[7,9,28],[12,17,9],[17,12,10],[30,26,16],[13,7,30],[17,2,30],[14,25,5],[9,31,24],[19,4,25],[12,6,18],[19,23,13],[23,3,27],[19,6,22],[0,9,1],[15,10,13],[12,2,10],[9,14,24],[8,11,18],[7,22,25],[21,5,2],[22,3,12],[11,6,24],[30,16,21],[30,25,4],[28,23,4],[30,1,26],[25,3,16],[19,20,13],[2,7,30],[4,27,20],[9,15,18],[15,27,10],[21,19,22],[12,6,21],[5,11,23],[8,4,27],[28,4,13],[13,5,28],[26,17,19],[18,28,11],[18,6,15],[31,23,16],[6,13,29],[15,5,8],[9,12,4],[24,4,22],[11,22,20],[30,21,6],[2,15,8],[18,23,10],[26,8,2],[0,23,27],[31,6,11],[12,30,2],[17,3,8],[11,1,21],[0,22,4],[22,3,6],[12,19,11],[11,6,2],[17,28,9],[27,21,10],[22,6,16],[15,23,0],[3,31,22],[22,14,8],[26,15,0],[28,5,27],[22,21,12],[3,22,15],[16,31,9],[11,29,16],[24,28,23],[27,20,1],[29,8,21],[3,25,17],[18,16,17],[23,22,28],[24,25,27],[6,2,14],[27,31,18],[16,11,12],[15,19,20],[19,14,13],[10,12,23],[0,6,18],[20,5,2],[19,31,29],[28,11,9],[7,19,22],[2,3,9],[4,7,26],[2,17,26],[15,24,13],[17,23,22],[19,18,5],[3,25,5],[29,20,3],[31,4,22],[31,27,13],[30,1,4],[6,20,10],[13,3,8],[8,17,16],[20,10,6],[5,9,12],[18,0,17],[5,20,25],[20,26,14],[19,31,4],[11,23,30],[10,28,21],[4,28,27],[16,27,24],[30,23,11],[8,22,1],[26,30,24],[17,19,25],[12,5,15],[5,25,7],[20,4,30],[12,9,27],[31,13,18],[31,11,26],[7,5,19],[9,28,6],[16,10,11],[29,19,9],[30,4,18],[20,9,7],[4,25,10],[22,8,26],[29,19,15],[9,28,18],[1,12,18],[10,11,14],[23,25,2],[21,4,24],[16,0,26],[14,31,11],[13,20,26],[25,29,4],[31,28,3],[14,6,10],[18,2,21],[17,6,24],[5,6,12],[6,11,9],[14,12,5],[0,26,15],[8,18,19],[16,20,31],[24,31,16],[31,21,10],[15,8,21],[20,23,14],[11,27,1],[3,13,20],[12,15,6],[2,18,19],[26,25,0],[31,3,21],[0,11,22],[11,12,7],[13,30,21],[15,4,28],[13,24,4],[29,21,6],[11,22,26]],[[25,1,17],[1,20,22],[13,4,30],[14,13,21],[25,1,15],[8,7,20],[7,27,4],[19,13,22],[28,26,31],[12,2,21],[17,24,2],[23,5,30],[30,13,6],[12,17,14],[4,22,25],[16,14,12],[1,7,3],[11,10,2],[22,29,24],[27,9,22],[3,14,1],[18,9,14],[29,2,25],[26,28,7],[20,1,10],[5,1,18],[3,0,19],[21,9,13],[17,6,20],[17,26,10],[4,17,5],[4,21,8],[18,10,14],[25,21,24],[10,1,20],[7,9,5],[21,25,13],[18,24,5],[9,16,25],[4,21,12],[3,15,20],[15,31,27],[14,30,12],[1,24,17],[15,5,30],[0,13,1],[10,15,8],[30,21,4],[0,16,5],[1,6,10],[15,9,20],[10,18,7],[10,8,20],[0,23,3],[9,6,17],[11,0,10],[27,21,1],[9,5,3],[0,19,8],[22,9,7],[15,13,22],[26,23,16],[15,2,25],[2,14,8],[13,5,9],[9,4,28],[3,27,16],[18,15,28],[10,16,26],[24,14,18],[5,1,0],[15,7,16],[6,3,11],[6,10,4],[19,18,27],[12,0,24],[10,0,26],[3,12,21],[20,3,21],[17,13,24],[20,30,29],[17,2,5],[30,14,4],[2,0,24],[1,30,31],[25,15,1],[8,28,31],[5,11,29],[3,7,14],[18,31,4],[6,30,22],[7,18,31],[25,26,22],[2,6,17],[2,3,20],[27,17,24],[20,21,3],[13,16,14],[23,3,10],[4,5,20],[13,26,29],[20,11,26],[22,25,27],[0,16,2],[16,9,13],[5,28,26],[20,23,0],[23,16,4],[28,27,7],[28,17,2],[3,19,13],[28,10,12],[9,28,8],[28,2,30],[14,1,0],[18,25,14],[27,4,28],[16,22,7],[29,31,10],[1,23,27],[3,16,17],[2,26,19],[4,7,30],[22,0,30],[23,16,18],[24,13,2],[2,15,10],[17,12,5],[9,24,7],[15,11,29],[13,20,3],[13,0,28],[25,8,3],[14,5,10],[20,25,6],[31,23,9],[0,7,18],[18,22,17],[6,19,29],[31,27,24],[20,19,0],[3,24,25],[1,19,9],[20,9,12],[5,27,8],[12,17,27],[23,27,1],[1,24,5],[18,2,22],[14,8,15],[4,2,7],[5,4,23],[8,28,7],[8,22,24],[7,5,11],[10,2,29],[7,22,27],[12,4,27],[10,5,24],[21,25,3],[29,26,23],[0,7,5],[17,22,13],[5,10,7],[1,15,8],[10,21,13],[2,14,21],[17,4,5],[3,22,2],[22,8,14],[30,2,22],[4,2,11],[17,26,20],[17,7,23],[31,14,11],[29,14,7],[28,22,9],[12,4,23],[21,6,7],[6,29,23],[3,11,15],[6,4,8],[7,23,18],[2,30,27],[2,12,17],[30,18,15],[12,10,11],[10,16,1],[9,8,22],[25,30,0],[29,1,11],[26,19,5],[25,4,16],[0,18,21],[11,0,16],[9,31,30],[15,27,31],[1,15,16],[26,22,24],[26,20,31],[28,30,20],[9,18,25],[11,1,10],[30,19,6],[25,4,31],[4,3,11],[27,20,9],[2,11,3],[1,0,28],[30,12,15],[11,8,9],[25,26,17],[30,2,24],[22,12,23],[3,10,4],[26,24,29],[31,3,0],[28,25,24],[18,28,12],[6,19,25],[0,28,2],[6,21,16],[20,10,13],[24,12,8],[10,30,19],[5,10,4],[31,26,10],[5,25,26],[17,15,4],[30,3,7],[25,20,8],[21,30,18],[16,6,7],[19,15,30],[22,2,31],[0,20,21],[5,13,18],[30,1,8],[4,21,17],[20,16,28],[27,18,1],[18,11,15],[15,24,10],[26,27,2],[28,14,17],[30,4,25],[14,8,16],[19,1,25],[22,21,26],[29,2,15],[17,23,11],[9,24,31],[18,25,24],[19,2,1],[31,19,30],[26,20,18]],[[7,12,29],[14,19,4],[30,9,12],[1,30,17],[28,27,11],[12,13,5],[5,16,1],[4,22,7],[23,1,27],[0,4,11],[2,24,7],[27,18,26],[29,4,22],[22,12,2],[27,11,23],[5,24,17],[9,4,22],[21,4,10],[14,31,3],[5,31,29],[28,17,23],[14,6,2],[0,20,6],[29,19,25],[6,4,16],[15,25,0],[9,5,8],[26,6,17],[28,23,11],[26,12,7],[18,31,13],[22,26,31],[3,15,21],[12,9,13],[14,31,25],[1,13,19],[29,13,5],[15,28,18],[6,9,14],[26,29,14],[23,5,30],[24,28,18],[12,8,19],[23,9,5],[30,3,27],[17,16,27],[7,10,12],[9,13,20],[21,24,25],[28,9,1],[6,23,13],[6,3,25],[8,30,1],[13,25,22],[29,25,24],[5,25,28],[27,17,14],[22,14,26],[5,24,28],[30,2,20],[8,19,15],[10,8,30],[7,16,19],[12,22,1],[24,18,15],[18,25,17],[30,3,7],[1,23,28],[11,25,10],[8,3,27],[26,11,2],[24,28,31],[1,19,15],[11,27,21],[22,23,25],[12,13,2],[17,23,29],[30,14,29],[17,29,6],[1,5,22],[0,4,9],[14,26,13],[20,21,13],[25,22,11],[27,28,12],[11,19,6],[2,12,8],[24,4,20],[26,0,11],[15,22,21],[3,4,0],[10,23,19],[1,28,0],[1,16,6],[14,8,10],[9,11,28],[12,25,4],[19,17,30],[26,31,22],[16,18,3],[26,10,5],[30,2,6],[26,12,0],[23,24,20],[29,17,16],[7,0,31],[3,2,16],[24,13,30],[24,28,29],[3,16,31],[14,31,16],[11,31,18],[27,11,12],[20,16,30],[23,15,31],[24,22,28],[29,27,7],[11,23,10],[17,1,18],[18,17,23],[31,24,12],[30,17,10],[21,23,24],[9,20,27],[25,23,27],[18,17,15],[24,17,16],[8,12,9],[17,31,26],[1,5,24],[22,12,10],[19,26,8],[30,20,16],[21,6,0],[12,6,10],[8,29,17],[13,10,1],[10,29,11],[5,23,21],[19,0,26],[6,19,21],[15,25,30],[2,25,18],[29,18,23],[25,14,17],[13,14,26],[11,9,1],[26,16,8],[30,25,11],[16,20,18],[28,23,19],[8,0,1],[19,26,10],[0,7,1],[18,29,31],[22,7,9],[0,4,2],[9,21,8],[26,1,6],[24,23,22],[8,22,26],[10,25,1],[5,0,21],[12,31,29],[12,16,31],[27,4,22],[13,26,16],[15,20,19],[18,29,5],[9,15,6],[12,15,30],[25,4,0],[20,13,8],[25,13,3],[14,9,6],[15,11,20],[7,18,26],[18,16,12],[27,28,2],[11,19,2],[4,21,26],[17,24,22],[13,29,1],[6,1,18],[3,23,5],[23,24,11],[25,28,27],[0,11,9],[3,25,11],[30,17,28],[19,2,28],[13,20,9],[3,29,26],[31,0,3],[9,29,10],[25,19,2],[10,15,5],[21,1,8],[18,7,15],[19,13,15],[21,9,24],[11,23,28],[15,7,2],[6,0,29],[24,15,22],[18,31,29],[29,5,28],[2,18,7],[25,22,21],[18,13,30],[22,29,30],[7,12,18],[0,13,22],[13,1,17],[29,5,19],[22,7,8],[18,20,17],[0,6,1],[15,23,30],[16,11,22],[19,11,28],[28,31,3],[20,25,16],[27,23,26],[22,12,7],[22,3,24],[13,11,7],[6,8,24],[17,27,26],[19,5,4],[12,17,11],[1,18,29],[15,28,18],[19,6,22],[1,16,30],[2,13,11],[0,12,26],[18,2,28],[4,0,20],[7,1,2],[31,2,30],[17,8,28],[28,22,9],[30,27,16],[3,21,10],[3,10,0],[12,5,10],[25,9,13],[3,26,9],[2,30,14],[21,1,18],[13,6,16],[31,14,18],[21,2,0],[4,13,12],[12,16,22]],[[16,0,14],[22,28,0],[26,30,18],[30,0,1],[29,1,28],[9,6,3],[15,13,28],[24,25,20],[24,13,2],[31,12,16],[29,6,30],[14,11,0],[12,27,10],[19,18,30],[17,26,25],[23,19,3],[18,20,27],[15,23,31],[15,2,19],[13,12,29],[30,1,29],[18,19,17],[28,8,23],[28,7,25],[19,16,30],[3,21,1],[26,3,18],[9,22,4],[4,27,11],[16,28,20],[12,4,6],[3,5,4],[14,23,13],[0,17,3],[19,8,16],[22,6,17],[1,8,12],[29,20,31],[6,26,8],[18,12,22],[11,2,4],[20,27,18],[15,21,9],[4,13,12],[9,4,25],[12,3,23],[11,17,9],[15,22,28],[1,13,9],[26,18,17],[10,4,16],[3,7,27],[13,1,26],[29,8,16],[3,14,25],[26,24,28],[22,10,18],[19,7,2],[10,0,26],[28,4,11],[19,25,11],[4,13,9],[2,26,7],[1,10,16],[29,27,17],[17,4,30],[24,26,2],[0,20,18],[7,19,5],[11,28,12],[31,8,16],[24,2,6],[11,2,19],[3,25,26],[24,8,31],[3,17,20],[31,20,28],[28,17,11],[1,28,7],[29,0,25],[25,10,5],[28,25,9],[21,10,22],[20,11,7],[23,16,17],[0,1,28],[22,24,13],[24,11,30],[30,3,27],[22,25,6],[10,3,7],[2,29,9],[24,16,29],[11,31,17],[28,25,27],[2,17,4],[14,3,4],[16,24,11],[25,7,22],[21,6,16],[20,0,24],[7,16,14],[13,6,23],[26,29,6],[16,10,12],[5,25,6],[30,20,24],[25,22,16],[27,17,9],[8,21,31],[13,2,1],[15,0,8],[22,10,15],[1,27,28],[14,20,10],[16,25,17],[16,8,27],[10,24,12],[21,28,18],[16,5,4],[4,8,9],[10,31,2],[3,19,8],[6,11,16],[20,21,9],[16,31,0],[22,26,28],[29,20,28],[26,21,24],[20,27,2],[12,13,23],[18,26,31],[17,19,28],[8,14,31],[25,7,1],[1,21,0],[2,20,4],[12,10,8],[8,28,15],[19,17,9],[28,0,8],[17,15,31],[6,9,7],[7,3,20],[22,29,4],[13,17,21],[31,10,21],[9,5,14],[25,6,18],[5,20,21],[7,6,30],[5,10,8],[8,24,30],[17,26,0],[27,10,2],[29,3,7],[4,30,17],[30,23,0],[21,16,18],[23,9,19],[27,23,10],[0,13,21],[15,30,23],[1,22,28],[27,9,26],[16,10,11],[16,10,25],[13,22,31],[27,28,10],[26,17,7],[9,21,13],[22,3,11],[28,7,13],[31,26,19],[15,30,18],[2,20,11],[16,24,15],[1,7,9],[7,21,1],[2,4,19],[15,23,1],[8,1,9],[19,21,25],[29,20,28],[17,16,31],[5,6,26],[22,1,3],[13,24,12],[31,30,21],[18,1,7],[18,20,14],[6,14,26],[18,0,21],[3,8,0],[10,1,28],[3,0,6],[19,3,10],[21,10,30],[22,2,5],[7,9,4],[9,21,12],[19,18,25],[8,21,14],[4,30,8],[7,17,26],[16,30,8],[20,14,24],[22,27,10],[22,26,0],[24,4,21],[11,21,4],[10,14,25],[15,12,23],[30,28,3],[3,4,27],[3,9,19],[21,10,9],[17,1,18],[17,6,15],[27,22,29],[24,12,3],[9,1,18],[30,24,15],[28,7,16],[6,12,19],[1,9,19],[4,0,30],[22,4,13],[6,9,26],[20,4,16],[13,16,25],[29,7,10],[5,24,12],[5,10,3],[5,6,28],[5,29,24],[17,5,18],[5,2,16],[2,25,1],[24,16,13],[11,21,5],[16,14,21],[24,17,6],[6,4,24],[1,25,28],[3,20,21],[20,16,29],[22,23,28],[3,31,21],[11,23,15],[27,29,7],[31,22,23],[15,4,19],[16,4,7],[25,14,1],[10,4,12]],[[14,27,1],[26,30,0],[24,23,11],[1,25,12],[31,10,5],[25,7,22],[6,5,12],[0,15,11],[13,29,30],[12,22,9],[3,8,20],[29,6,13],[11,28,9],[22,23,11],[30,13,2],[17,23,15],[4,25,12],[11,22,26],[15,7,26],[28,6,9],[29,6,5],[6,10,27],[30,10,9],[3,5,14],[19,21,3],[31,26,14],[4,27,21],[5,6,17],[8,31,19],[3,30,23],[19,28,20],[26,14,4],[30,12,19],[2,21,0],[3,23,14],[18,1,23],[23,0,6],[16,12,21],[25,24,20],[24,7,22],[0,8,11],[6,8,30],[16,25,19],[9,5,12],[18,1,9],[24,1,6],[19,25,23],[18,29,19],[15,18,9],[26,30,15],[13,2,30],[13,14,21],[23,17,3],[1,6,20],[6,13,9],[17,18,7],[4,24,17],[17,0,27],[11,7,23],[11,30,5],[22,26,10],[17,6,28],[6,31,24],[21,5,12],[12,20,22],[5,26,4],[9,16,28],[0,6,17],[9,18,2],[16,9,7],[22,16,30],[18,10,15],[18,29,16],[19,31,5],[23,28,5],[13,21,12],[7,18,6],[22,16,3],[15,30,2],[5,19,3],[21,1,10],[20,13,6],[24,12,31],[14,2,23],[7,28,6],[4,11,13],[4,11,12],[13,9,5],[25,12,29],[9,21,23],[7,11,4],[14,3,7],[2,14,28],[20,19,10],[8,2,0],[29,31,19],[24,15,29],[26,9,12],[31,20,13],[13,5,20],[9,3,7],[6,3,27],[15,7,8],[29,27,17],[18,29,22],[6,20,2],[24,12,14],[29,19,22],[16,13,6],[20,14,7],[21,7,10],[27,20,22],[28,30,13],[29,7,2],[14,0,31],[19,24,26],[15,17,23],[16,31,7],[16,18,22],[9,27,20],[25,21,17],[30,16,31],[28,18,14],[8,23,2],[6,23,3],[7,25,0],[14,4,6],[15,20,19],[20,12,19],[2,28,14],[0,15,21],[23,10,28],[1,25,4],[3,17,4],[30,18,23],[16,22,6],[17,9,27],[20,25,27],[10,25,30],[31,13,24],[16,18,24],[16,7,17],[10,17,8],[12,4,8],[20,27,24],[12,26,22],[16,14,11],[31,17,9],[27,7,30],[12,18,11],[27,20,13],[4,29,26],[25,16,7],[24,27,21],[13,27,30],[0,1,7],[3,27,19],[24,27,17],[9,1,11],[2,17,16],[27,24,4],[12,6,13],[24,28,11],[0,31,24],[30,22,28],[23,19,22],[14,7,17],[25,20,8],[11,9,27],[18,14,1],[31,6,28],[18,9,29],[27,28,1],[14,16,6],[17,18,10],[10,22,25],[22,13,18],[7,25,13],[4,7,15],[25,20,17],[2,29,26],[14,0,30],[14,25,1],[19,9,4],[11,3,17],[31,5,20],[26,15,5],[21,9,24],[6,9,3],[12,28,18],[8,28,3],[9,14,12],[22,18,9],[17,30,31],[7,16,14],[22,15,10],[26,21,29],[15,12,22],[1,2,11],[10,17,11],[18,20,15],[8,10,11],[25,4,1],[30,5,21],[19,0,28],[25,2,8],[2,1,13],[18,16,28],[21,12,23],[12,29,28],[9,8,24],[3,16,28],[6,0,19],[3,19,30],[20,23,22],[13,28,26],[1,15,29],[3,5,16],[30,7,27],[18,11,31],[17,12,24],[2,29,23],[9,28,31],[0,17,13],[18,0,16],[26,9,1],[31,29,12],[0,14,8],[17,24,20],[8,28,24],[13,9,16],[30,6,8],[23,1,12],[12,11,18],[15,9,3],[12,28,22],[19,28,17],[9,8,24],[30,9,6],[20,17,27],[10,18,17],[13,10,8],[14,30,7],[8,27,15],[28,16,8],[31,30,3],[7,14,3],[1,20,11],[8,7,15],[15,22,2],[30,24,20],[24,17,22],[11,16,24],[27,23,24],[31,15,19],[7,24,29]],[[3,2,22],[12,17,13],[0,12,16],[14,13,19],[18,23,26],[11,24,20],[11,12,16],[28,11,16],[29,15,9],[14,15,26],[12,26,25],[19,3,7],[18,13,11],[31,22,17],[3,27,23],[9,18,5],[24,23,19],[23,21,6],[7,31,9],[18,16,7],[17,27,6],[29,15,1],[15,12,6],[14,11,27],[30,18,5],[27,16,2],[19,17,22],[30,5,2],[15,16,7],[22,3,21],[0,4,10],[12,17,2],[0,25,3],[6,16,20],[24,9,19],[26,24,7],[29,9,7],[22,0,7],[17,3,13],[0,27,10],[2,0,15],[13,6,22],[13,18,6],[10,30,25],[14,27,22],[30,9,6],[22,17,14],[31,11,5],[25,4,11],[18,30,24],[2,15,7],[18,15,26],[28,19,23],[3,21,17],[18,20,13],[6,20,13],[8,9,12],[5,27,10],[31,9,17],[31,25,4],[31,18,16],[31,21,12],[22,6,16],[23,17,8],[29,11,23],[5,13,12],[4,20,18],[22,31,3],[29,10,13],[0,19,16],[4,23,0],[29,8,14],[13,20,30],[21,14,2],[10,2,3],[6,7,15],[1,19,7],[16,19,6],[16,15,9],[0,21,28],[16,7,8],[30,19,14],[22,7,25],[14,10,6],[31,16,10],[22,14,1],[24,22,23],[9,24,25],[27,1,5],[14,2,18],[22,2,1],[16,4,17],[19,5,14],[22,27,26],[29,4,0],[13,16,23],[9,22,6],[24,0,21],[28,8,27],[23,18,19],[12,23,20],[12,26,1],[6,15,4],[17,6,16],[15,13,10],[12,27,18],[0,31,15],[20,29,9],[11,25,24],[28,25,27],[27,31,11],[6,31,23],[18,27,29],[27,18,28],[6,23,5],[25,13,15],[7,21,25],[23,4,21],[2,20,4],[5,9,1],[9,28,8],[15,21,9],[25,18,12],[1,28,30],[7,3,0],[6,23,25],[22,31,1],[7,2,5],[27,20,21],[19,16,5],[4,22,29],[31,28,9],[26,12,5],[21,10,23],[24,0,13],[17,28,6],[7,8,13],[29,6,25],[11,30,21],[31,27,20],[15,9,27],[21,8,6],[3,8,5],[17,19,18],[16,2,3],[10,29,26],[8,18,4],[3,0,24],[4,8,16],[16,27,12],[7,31,17],[11,31,14],[19,5,29],[27,5,19],[29,8,12],[7,22,14],[26,5,19],[20,28,27],[6,23,28],[24,14,18],[29,23,18],[28,15,1],[20,4,0],[15,26,11],[29,28,2],[16,11,2],[20,17,7],[14,4,24],[1,10,18],[6,15,28],[27,26,17],[2,26,17],[2,11,19],[29,8,20],[10,1,6],[16,2,1],[19,28,16],[10,25,11],[25,0,16],[16,28,19],[14,7,30],[25,19,18],[14,10,29],[13,25,31],[15,3,23],[27,20,19],[26,1,31],[23,7,29],[12,2,30],[19,4,15],[2,21,7],[30,12,29],[0,17,20],[9,18,22],[6,2,16],[21,27,31],[16,21,11],[3,30,21],[12,27,29],[3,17,0],[7,2,21],[3,8,13],[0,6,23],[2,23,3],[19,0,28],[29,10,8],[12,30,10],[24,0,23],[25,17,20],[16,27,14],[5,30,14],[10,11,31],[9,5,31],[4,25,21],[11,1,18],[13,25,24],[1,5,22],[2,6,1],[10,19,9],[21,5,27],[25,8,30],[1,24,3],[27,29,8],[0,28,18],[23,31,13],[7,15,1],[16,19,31],[2,19,8],[5,17,28],[17,11,30],[12,16,24],[14,24,10],[21,20,11],[6,4,1],[18,2,26],[25,12,21],[26,3,31],[21,23,30],[11,8,21],[16,19,17],[3,0,20],[29,21,16],[3,14,23],[4,15,14],[30,23,25],[3,4,31],[15,8,22],[18,16,26],[19,10,28],[0,12,7],[13,9,3],[12,29,7],[11,8,28],[12,11,14],[30,12,18],[3,26,28]],[[29,17,18],[17,10,27],[8,16,13],[12,22,13],[30,21,6],[5,26,28],[16,13,23],[31,25,21],[24,9,13],[15,23,9],[23,5,7],[8,5,6],[25,3,19],[30,13,23],[28,26,3],[19,18,30],[10,19,23],[11,19,1],[19,29,10],[23,10,2],[13,27,26],[4,24,25],[26,31,29],[6,14,17],[30,7,27],[0,13,27],[24,9,11],[8,18,31],[8,7,1],[1,6,0],[1,17,6],[2,18,26],[29,30,26],[7,24,23],[18,27,5],[14,24,27],[21,31,10],[18,31,26],[14,10,11],[26,16,24],[17,8,14],[3,13,1],[10,21,24],[6,9,8],[7,8,28],[15,0,1],[13,10,9],[19,30,5],[1,23,19],[5,21,27],[22,8,31],[27,3,7],[22,19,13],[4,20,15],[16,19,7],[12,20,14],[5,3,6],[25,22,26],[2,15,19],[12,24,19],[7,17,2],[1,23,24],[28,15,6],[15,21,26],[0,4,18],[8,29,9],[31,3,26],[4,25,3],[7,29,20],[29,1,9],[6,14,30],[6,1,29],[17,16,24],[19,14,28],[27,30,31],[2,23,27],[14,5,26],[16,8,30],[28,27,24],[9,8,10],[28,25,19],[25,9,20],[27,15,17],[2,11,12],[26,30,23],[30,19,29],[28,9,29],[11,16,18],[28,5,21],[16,28,29],[30,13,6],[28,19,15],[9,7,3],[7,8,17],[9,19,1],[30,6,0],[28,14,7],[15,11,26],[2,12,4],[12,15,1],[22,25,26],[17,8,0],[10,23,30],[21,18,0],[26,21,30],[28,18,26],[1,17,12],[23,13,27],[23,20,29],[8,7,20],[7,21,30],[3,26,24],[4,3,13],[28,18,7],[12,31,9],[18,6,24],[24,7,29],[20,1,31],[14,12,18],[20,26,4],[9,8,10],[10,6,2],[28,10,7],[19,20,11],[19,30,14],[13,2,5],[26,4,12],[3,6,2],[1,21,23],[21,23,6],[19,8,14],[7,21,25],[24,5,10],[6,30,14],[18,1,24],[13,19,26],[8,17,31],[5,6,2],[17,11,29],[22,20,29],[20,17,3],[30,23,20],[0,31,28],[19,12,23],[18,28,12],[9,26,1],[0,18,27],[24,14,25],[2,16,23],[17,10,29],[10,29,30],[27,14,9],[29,30,11],[18,14,16],[17,13,6],[3,13,17],[19,6,4],[4,21,14],[25,4,11],[16,22,15],[1,20,11],[13,0,27],[7,18,5],[8,21,13],[14,28,20],[25,6,20],[28,15,23],[29,14,10],[31,29,27],[19,7,21],[13,7,23],[8,2,5],[9,20,24],[2,1,28],[8,6,3],[5,8,7],[8,13,14],[26,15,0],[5,1,0],[23,25,3],[23,22,6],[30,14,1],[1,17,6],[2,5,12],[16,8,19],[29,17,27],[29,24,9],[22,24,5],[0,20,11],[13,18,30],[0,24,11],[3,30,15],[28,1,19],[1,16,7],[13,4,22],[26,29,8],[30,2,31],[27,29,0],[10,30,13],[0,14,6],[25,19,2],[4,27,7],[8,25,5],[3,19,4],[9,28,13],[15,4,23],[0,3,15],[12,3,21],[18,4,29],[11,2,8],[16,13,15],[24,12,18],[11,20,15],[1,29,31],[15,2,4],[6,27,12],[24,5,22],[9,30,11],[24,11,23],[12,14,0],[0,1,21],[16,0,28],[1,22,14],[1,17,0],[31,28,21],[22,19,12],[25,16,18],[25,18,9],[3,25,20],[11,2,4],[6,19,13],[30,12,16],[16,8,30],[25,28,16],[5,21,2],[27,23,10],[13,9,10],[11,12,0],[24,18,26],[9,2,21],[9,8,7],[18,19,7],[9,10,31],[13,17,20],[16,31,1],[5,15,21],[27,5,10],[24,30,6],[4,0,16],[8,10,6],[12,31,9],[31,22,20],[29,19,22],[26,19,28],[8,2,24],[6,4,27]],[[7,23,22],[9,8,15],[18,21,12],[26,12,29],[18,0,5],[20,24,11],[9,4,18],[13,1,31],[22,13,30],[5,8,16],[30,22,19],[13,20,17],[24,8,19],[27,15,16],[4,11,5],[28,27,10],[2,28,12],[4,2,11],[10,29,27],[15,21,5],[29,27,25],[0,29,7],[22,0,18],[11,30,13],[6,0,31],[27,29,0],[5,13,20],[10,26,29],[10,9,7],[30,6,2],[15,6,8],[31,12,1],[23,28,8],[28,13,16],[17,11,16],[8,6,7],[10,19,14],[29,13,2],[0,18,15],[18,27,29],[16,10,5],[8,15,0],[21,5,25],[6,2,4],[8,3,10],[16,19,6],[24,20,2],[26,31,9],[0,12,20],[25,12,17],[26,6,28],[0,4,7],[11,29,0],[3,17,5],[23,22,20],[30,19,25],[3,18,20],[1,8,5],[21,10,8],[23,24,26],[28,4,9],[22,5,25],[12,7,17],[29,9,27],[14,16,31],[29,20,26],[14,2,12],[0,31,29],[15,2,24],[10,27,21],[5,26,7],[31,24,0],[27,25,10],[14,6,1],[8,27,26],[26,30,7],[26,6,15],[7,24,30],[28,14,21],[24,4,17],[25,24,18],[2,17,18],[28,11,23],[1,31,5],[2,1,19],[27,0,11],[0,25,18],[15,30,8],[23,18,11],[14,9,22],[7,1,27],[19,14,15],[3,19,23],[23,14,3],[27,13,9],[26,15,2],[25,18,15],[28,2,25],[29,27,22],[20,28,6],[0,9,20],[6,26,17],[0,24,23],[8,17,16],[1,8,25],[11,27,10],[3,31,17],[22,1,23],[18,28,26],[20,27,24],[19,27,4],[12,25,18],[8,24,14],[11,5,3],[6,21,20],[17,2,18],[23,26,31],[19,31,24],[31,17,20],[9,10,2],[30,12,2],[25,0,18],[18,0,19],[17,1,25],[11,14,9],[7,27,10],[29,4,17],[20,7,8],[2,25,0],[3,26,20],[22,19,20],[4,29,27],[24,0,27],[7,13,23],[2,30,5],[10,22,25],[30,26,27],[4,2,8],[1,25,13],[26,29,0],[31,25,16],[5,6,25],[25,28,2],[10,15,6],[19,2,15],[5,31,16],[7,19,28],[2,1,28],[28,1,15],[12,20,29],[28,15,26],[9,3,31],[27,21,11],[21,22,3],[5,8,4],[0,3,7],[27,17,8],[19,10,4],[10,15,1],[11,2,29],[3,24,31],[4,15,0],[17,7,27],[24,5,29],[19,24,10],[28,25,2],[18,1,7],[29,14,19],[12,15,25],[16,11,28],[21,0,11],[14,27,17],[6,27,14],[5,11,28],[31,22,5],[19,25,21],[10,0,1],[19,31,13],[12,24,6],[11,4,6],[2,28,15],[1,27,24],[18,12,30],[8,27,29],[1,19,4],[26,30,12],[9,21,10],[27,4,31],[14,0,3],[12,19,6],[16,20,25],[25,29,17],[15,26,17],[27,19,9],[6,21,27],[14,1,21],[19,9,14],[20,25,15],[20,3,28],[31,12,18],[19,29,25],[7,26,22],[12,2,18],[10,29,13],[2,7,3],[12,11,1],[25,11,26],[24,11,17],[9,6,3],[23,13,16],[15,24,26],[18,8,21],[28,23,8],[0,9,17],[9,4,18],[7,25,4],[5,7,21],[4,25,26],[24,12,30],[25,13,20],[18,10,16],[10,22,15],[3,7,16],[23,2,16],[15,25,3],[27,7,19],[16,11,3],[24,0,29],[0,19,22],[16,14,11],[4,28,0],[31,2,22],[16,17,19],[9,3,17],[3,12,4],[6,18,0],[4,19,10],[3,22,15],[31,22,5],[10,27,17],[28,18,12],[20,16,30],[14,24,2],[14,18,11],[9,16,28],[4,5,29],[7,12,28],[1,16,27],[7,9,27],[15,5,14],[2,3,30],[6,21,30],[10,2,8],[6,17,13],[24,20,16],[11,14,5]]]
ZW = 825
def setup_inputs(rng):
    return {"z": rng.standard_normal((N, 128, ZW), dtype=np.float32), "g": rng.random((N, 128, T * K), dtype=np.float32)}
def reference(z, g):
    y = np.zeros((N, 128, T), np.float64)
    fill = [0] * N
    for r in range(N):
        for t in range(T):
            for k, e in enumerate(ROUTE[r][t]):
                y[r][:, t] += g[r][:, t * K + k].astype(np.float64) * z[e][:, fill[e]].astype(np.float64)
                fill[e] += 1
    return {"y": y.astype(z.dtype)}

@@ -1,0 +1,106 @@
+from concourse.mybir import AluOpType
+
+SCRATCH = {
+    "zs": ("sbuf", [128, 825], "float32"),
+    "gs": ("sbuf", [128, 768], "float32"),
+    "cab": ("sbuf", [128, 424], "float32"),
+    "land": ("sbuf", [128, 768], "float32"),
+    "w": ("sbuf", [128, 768], "float32"),
+    "acc": ("sbuf", [128, 256], "float32"),
+    "ys": ("sbuf", [128, 256], "float32"),
+}
+SEMAPHORES = ["zl", "gl", "cabarr", "arrived", "sent", "vs", "va", "vdone", "stored"]
+
+
+def rank_program(g, core, T, topo):
+    me = T.rank_of(core)
+    if me is None:
+        return
+    cores = T.cores
+    n = len(cores)
+    route = T.tables["ROUTE"]
+    nt, nk = T.tables["T"], T.tables["K"]
+    pos = [[[] for _ in range(n)] for _ in range(n)]
+    for r in range(n):
+        for t in range(nt):
+            for k in range(nk):
+                pos[route[r][t][k]][r].append(t * nk + k)
+    cnt = [[len(pos[e][r]) for r in range(n)] for e in range(n)]
+
+    def zoff(e, r):
+        return sum(cnt[e][:r])
+
+    def loff(r, e):
+        return sum(cnt[x][r] for x in range(e))
+
+    sem = T.sem
+    my_rack = me // 16
+    partner = (3 - me // 8) * 8 + me % 8
+    far0 = (1 - my_rack) * 16
+    near0 = my_rack * 16
+
+    g.sync.dma_start(T.zs[:], T.z[:]).then_inc(sem.zl, 16)
+    g.scalar.dma_start(T.gs[:], T.g[:]).then_inc(sem.gl, 16)
+
+    nsent = 0
+
+    def send(dst_rank, out_ap, in_ap, rsem):
+        rid, pid = topo.addr(cores[dst_rank], core)
+        g.remote_dma(out_ap, in_ap, rsem, sem.sent, pid, rid, 0x00FF)
+
+    g.wait_ge(sem.zl, 16)
+    a, b = zoff(me, far0), zoff(me, far0 + 16)
+    send(partner, T.cab[:, 0:b - a], T.zs[:, a:b], sem.cabarr)
+    nsent += 8
+    for d in range(1, 16):
+        r = near0 + (me - near0 + d) % 16
+        a = zoff(me, r)
+        o = loff(r, me)
+        send(r, T.land[:, o:o + cnt[me][r]], T.zs[:, a:a + cnt[me][r]], sem.arrived)
+        nsent += 8
+    g.wait_ge(sem.cabarr, 8)
+    base = zoff(partner, near0)
+    for d in range(1, 16):
+        r = near0 + (me - near0 + d) % 16
+        a = zoff(partner, r) - base
+        o = loff(r, partner)
+        send(r, T.land[:, o:o + cnt[partner][r]], T.cab[:, a:a + cnt[partner][r]], sem.arrived)
+        nsent += 8
+    g.wait_ge(sem.sent, nsent)
+    g.wait_ge(sem.arrived, 240)
+
+    v = g.vector
+    nmul = [0]
+
+    def weigh(buf, off, cols):
+        i = 0
+        while i < len(cols):
+            j = i
+            step = 1
+            if i + 1 < len(cols):
+                step = cols[i + 1] - cols[i]
+                j = i + 1
+                while j + 1 < len(cols) and cols[j + 1] - cols[j] == step:
+                    j += 1
+            sl = slice(cols[i], cols[j] + 1, step)
+            v.tensor_tensor(T.w[:, sl], buf[:, off + i:off + j + 1], T.gs[:, sl], AluOpType.mult).then_inc(sem.vs, 1)
+            nmul[0] += 1
+            i = j + 1
+
+    v.wait_ge(sem.gl, 16)
+    v.wait_ge(sem.zl, 16)
+    weigh(T.zs, zoff(me, me), pos[me][me])
+    v.wait_ge(sem.cabarr, 8)
+    weigh(T.cab, zoff(partner, me) - base, pos[partner][me])
+    v.wait_ge(sem.arrived, 240)
+    for e in range(n):
+        if e != me and e != partner:
+            weigh(T.land, loff(me, e), pos[e][me])
+    v.wait_ge(sem.vs, nmul[0])
+    w = nt * nk
+    v.tensor_tensor(T.acc[:], T.w[:, 0:w:nk], T.w[:, 1:w:nk], AluOpType.add).then_inc(sem.va, 1)
+    v.wait_ge(sem.va, 1)
+    v.tensor_tensor(T.ys[:], T.acc[:], T.w[:, 2:w:nk], AluOpType.add).then_inc(sem.vdone, 1)
+    g.sync.wait_ge(sem.vdone, 1)
+    g.sync.dma_start(T.y[:], T.ys[:]).then_inc(sem.stored, 16)
+    g.sync.wait_ge(sem.stored, 16)

@@ -3,21 +3,22 @@ from concourse.mybir import AluOpType
 SCRATCH = {
     "zs": ("sbuf", [128, 825], "float32"),
     "gs": ("sbuf", [128, 768], "float32"),
-    "cab": ("sbuf", [128, 424], "float32"),
     "land": ("sbuf", [128, 768], "float32"),
-    "w": ("sbuf", [128, 768], "float32"),
-    "acc": ("sbuf", [128, 256], "float32"),
     "ys": ("sbuf", [128, 256], "float32"),
 }
-SEMAPHORES = ["zl", "gl", "cabarr", "arrived", "sent", "vs", "va", "vdone", "stored"]
+SEMAPHORES = ["zl", "gl", "hin", "fin", "near", "far", "sent", "vs", "va", "vdone", "stored"]
+
+CHIP, OFF = 0xFFFF, 0x00FF
 
 
 def rank_program(g, core, T, topo):
-    me = T.rank_of(core)
-    if me is None:
-        return
     cores = T.cores
     n = len(cores)
+    lc = core % 8
+    if topo.chip(core) >= 8 or lc in (1, 5):
+        return
+    chip0 = core - lc
+    me = T.rank_of(chip0 + 6)
     route = T.tables["ROUTE"]
     nt, nk = T.tables["T"], T.tables["K"]
     pos = [[[] for _ in range(n)] for _ in range(n)]
@@ -33,41 +34,77 @@ def rank_program(g, core, T, topo):
     def loff(r, e):
         return sum(cnt[x][r] for x in range(e))
 
+    def partner(s):
+        return (3 - s // 8) * 8 + s % 8
+
+    def chunks(s):
+        far0 = 16 * (1 - s // 16)
+        out = []
+        for half, senders in ((far0, (0, 2)), (far0 + 8, (4, 6))):
+            a, b = zoff(s, half), zoff(s, half + 8)
+            fwd = 2 if half // 8 == partner(s) // 8 else 3
+            out.append((senders[0], fwd, a, (a + b) // 2))
+            out.append((senders[1], fwd, (a + b) // 2, b))
+        return out
+
+    def cbase(s):
+        return zoff(s, 16 * (1 - s // 16))
+
     sem = T.sem
-    my_rack = me // 16
-    partner = (3 - me // 8) * 8 + me % 8
-    far0 = (1 - my_rack) * 16
-    near0 = my_rack * 16
+    nsent = [0]
+
+    def write(dst, out_ap, in_ap, rsem):
+        rid, pid = topo.addr(dst, core)
+        mask = CHIP if dst - dst % 8 == chip0 else OFF
+        g.remote_dma(out_ap, in_ap, rsem, sem.sent, pid, rid, mask)
+        nsent[0] += 16 if mask == CHIP else 8
+
+    def cable(c):
+        a, b = c[2] - cbase(me), c[3] - cbase(me)
+        write(cores[partner(me)] - 6 + c[1], T.land[:, a:b], T.zs[:, c[2]:c[3]], sem.fin)
+
+    def block(src, r, buf, col, rsem):
+        w = cnt[src][r]
+        o = loff(r, src)
+        write(cores[r], T.land[:, o:o + w], buf[:, col:col + w], rsem)
+
+    host0 = me - me % 8
+    other0 = host0 ^ 8
+    turn = [(me % 8 + d) % 8 for d in range(8)]
+
+    if lc in (0, 2, 4):
+        g.wait_ge(sem.hin, 16)
+        for c in chunks(me):
+            if c[0] == lc:
+                cable(c)
+    if lc == 7:
+        g.wait_ge(sem.hin, 16)
+        for d in turn:
+            block(me, other0 + d, T.zs, zoff(me, other0 + d), sem.near)
+    if lc in (2, 3):
+        src = partner(me)
+        g.wait_ge(sem.fin, 16)
+        for d in turn[1:] + turn[:1]:
+            r = (host0 if lc == 2 else other0) + d
+            block(src, r, T.land, zoff(src, r) - cbase(src), sem.far)
+    if lc != 6:
+        g.wait_ge(sem.sent, nsent[0])
+        return
 
     g.sync.dma_start(T.zs[:], T.z[:]).then_inc(sem.zl, 16)
     g.scalar.dma_start(T.gs[:], T.g[:]).then_inc(sem.gl, 16)
-
-    nsent = 0
-
-    def send(dst_rank, out_ap, in_ap, rsem):
-        rid, pid = topo.addr(cores[dst_rank], core)
-        g.remote_dma(out_ap, in_ap, rsem, sem.sent, pid, rid, 0x00FF)
-
     g.wait_ge(sem.zl, 16)
-    a, b = zoff(me, far0), zoff(me, far0 + 16)
-    send(partner, T.cab[:, 0:b - a], T.zs[:, a:b], sem.cabarr)
-    nsent += 8
-    for d in range(1, 16):
-        r = near0 + (me - near0 + d) % 16
-        a = zoff(me, r)
-        o = loff(r, me)
-        send(r, T.land[:, o:o + cnt[me][r]], T.zs[:, a:a + cnt[me][r]], sem.arrived)
-        nsent += 8
-    g.wait_ge(sem.cabarr, 8)
-    base = zoff(partner, near0)
-    for d in range(1, 16):
-        r = near0 + (me - near0 + d) % 16
-        a = zoff(partner, r) - base
-        o = loff(r, partner)
-        send(r, T.land[:, o:o + cnt[partner][r]], T.cab[:, a:a + cnt[partner][r]], sem.arrived)
-        nsent += 8
-    g.wait_ge(sem.sent, nsent)
-    g.wait_ge(sem.arrived, 240)
+    for c in chunks(me):
+        if c[0] != 6:
+            write(chip0 + c[0], T.zs[:, c[2]:c[3]], T.zs[:, c[2]:c[3]], sem.hin)
+    for c in chunks(me):
+        if c[0] == 6:
+            cable(c)
+    a, b = zoff(me, other0), zoff(me, other0 + 8)
+    write(chip0 + 7, T.zs[:, a:b], T.zs[:, a:b], sem.hin)
+    for d in turn[1:]:
+        block(me, host0 + d, T.zs, zoff(me, host0 + d), sem.near)
+    g.wait_ge(sem.sent, nsent[0])
 
     v = g.vector
     nmul = [0]
@@ -83,24 +120,26 @@ def rank_program(g, core, T, topo):
                 while j + 1 < len(cols) and cols[j + 1] - cols[j] == step:
                     j += 1
             sl = slice(cols[i], cols[j] + 1, step)
-            v.tensor_tensor(T.w[:, sl], buf[:, off + i:off + j + 1], T.gs[:, sl], AluOpType.mult).then_inc(sem.vs, 1)
+            v.tensor_tensor(T.gs[:, sl], buf[:, off + i:off + j + 1], T.gs[:, sl], AluOpType.mult).then_inc(sem.vs, 1)
             nmul[0] += 1
             i = j + 1
 
+    near0 = 16 * (me // 16)
     v.wait_ge(sem.gl, 16)
     v.wait_ge(sem.zl, 16)
     weigh(T.zs, zoff(me, me), pos[me][me])
-    v.wait_ge(sem.cabarr, 8)
-    weigh(T.cab, zoff(partner, me) - base, pos[partner][me])
-    v.wait_ge(sem.arrived, 240)
-    for e in range(n):
-        if e != me and e != partner:
+    v.wait_ge(sem.near, 15 * 8)
+    for e in range(near0, near0 + 16):
+        if e != me:
             weigh(T.land, loff(me, e), pos[e][me])
+    v.wait_ge(sem.far, 15 * 8 + 16)
+    for e in range(16 - near0, 32 - near0):
+        weigh(T.land, loff(me, e), pos[e][me])
     v.wait_ge(sem.vs, nmul[0])
     w = nt * nk
-    v.tensor_tensor(T.acc[:], T.w[:, 0:w:nk], T.w[:, 1:w:nk], AluOpType.add).then_inc(sem.va, 1)
+    v.tensor_tensor(T.ys[:], T.gs[:, 0:w:nk], T.gs[:, 1:w:nk], AluOpType.add).then_inc(sem.va, 1)
     v.wait_ge(sem.va, 1)
-    v.tensor_tensor(T.ys[:], T.acc[:], T.w[:, 2:w:nk], AluOpType.add).then_inc(sem.vdone, 1)
+    v.tensor_tensor(T.ys[:], T.ys[:], T.gs[:, 2:w:nk], AluOpType.add).then_inc(sem.vdone, 1)
     g.sync.wait_ge(sem.vdone, 1)
     g.sync.dma_start(T.y[:], T.ys[:]).then_inc(sem.stored, 16)
     g.sync.wait_ge(sem.stored, 16)

@@ -9,48 +9,99 @@ SCRATCH = {
 SEMAPHORES = ["zl", "gl", "hin", "fin", "near", "far", "sent", "vs", "va", "vdone", "stored"]
 
 CHIP, OFF = 0xFFFF, 0x00FF
+CACHE = {}
+
+
+def partner(s):
+    return (3 - s // 8) * 8 + s % 8
+
+
+def balance(cnt):
+    n = len(cnt)
+
+    def cost(swap):
+        load = {}
+
+        def wr(x, die, r, c):
+            at = x
+            if x % 2 != r % 2:
+                load[("m", x, die)] = load.get(("m", x, die), 0) + c
+                at = x ^ 1
+            if at != r:
+                load[("o", at, die)] = load.get(("o", at, die), 0) + c
+                load[("i", r, die)] = load.get(("i", r, die), 0) + c
+
+        for x in range(n):
+            own, oth, s = x - x % 8, (x - x % 8) ^ 8, partner(x)
+            for d in range(8):
+                if own + d != x:
+                    wr(x, 0, own + d, cnt[x][own + d])
+                    wr(x, 1, own + d, cnt[s][own + d])
+                wr(x, swap[x], oth + d, cnt[x][oth + d])
+                wr(x, 1 - swap[x], oth + d, cnt[s][oth + d])
+        return sum(v * v for v in load.values())
+
+    swap = [0] * n
+    best = cost(swap)
+    better = True
+    while better:
+        better = False
+        for x in range(n):
+            swap[x] ^= 1
+            c = cost(swap)
+            if c < best:
+                best, better = c, True
+            else:
+                swap[x] ^= 1
+    return swap
+
+
+def plan(T):
+    if "plan" not in CACHE:
+        n = len(T.cores)
+        route, nt, nk = T.tables["ROUTE"], T.tables["T"], T.tables["K"]
+        pos = [[[] for _ in range(n)] for _ in range(n)]
+        for r in range(n):
+            for t in range(nt):
+                for k in range(nk):
+                    pos[route[r][t][k]][r].append(t * nk + k)
+        cnt = [[len(pos[e][r]) for r in range(n)] for e in range(n)]
+        zoff = [[sum(cnt[e][:r]) for r in range(n + 1)] for e in range(n)]
+        loff = [[sum(cnt[x][r] for x in range(e)) for e in range(n + 1)] for r in range(n)]
+        CACHE["plan"] = (pos, cnt, zoff, loff, balance(cnt))
+    return CACHE["plan"]
 
 
 def rank_program(g, core, T, topo):
     cores = T.cores
-    n = len(cores)
     lc = core % 8
     if topo.chip(core) >= 8 or lc in (1, 5):
         return
     chip0 = core - lc
     me = T.rank_of(chip0 + 6)
-    route = T.tables["ROUTE"]
+    pos, cnt, zoff, loff, swap = plan(T)
     nt, nk = T.tables["T"], T.tables["K"]
-    pos = [[[] for _ in range(n)] for _ in range(n)]
-    for r in range(n):
-        for t in range(nt):
-            for k in range(nk):
-                pos[route[r][t][k]][r].append(t * nk + k)
-    cnt = [[len(pos[e][r]) for r in range(n)] for e in range(n)]
+    sem = T.sem
 
-    def zoff(e, r):
-        return sum(cnt[e][:r])
+    def neighbour(s):
+        return 3 if swap[s] else 7
 
-    def loff(r, e):
-        return sum(cnt[x][r] for x in range(e))
+    def forward(s):
+        return 7 if swap[s] else 3
 
-    def partner(s):
-        return (3 - s // 8) * 8 + s % 8
+    def cbase(s):
+        return zoff[s][16 * (1 - s // 16)]
 
     def chunks(s):
         far0 = 16 * (1 - s // 16)
         out = []
         for half, senders in ((far0, (0, 2)), (far0 + 8, (4, 6))):
-            a, b = zoff(s, half), zoff(s, half + 8)
-            fwd = 2 if half // 8 == partner(s) // 8 else 3
-            out.append((senders[0], fwd, a, (a + b) // 2))
-            out.append((senders[1], fwd, (a + b) // 2, b))
+            a, b = zoff[s][half], zoff[s][half + 8]
+            to = 2 if half // 8 == partner(s) // 8 else forward(partner(s))
+            out.append((senders[0], to, a, (a + b) // 2))
+            out.append((senders[1], to, (a + b) // 2, b))
         return out
 
-    def cbase(s):
-        return zoff(s, 16 * (1 - s // 16))
-
-    sem = T.sem
     nsent = [0]
 
     def write(dst, out_ap, in_ap, rsem):
@@ -65,7 +116,7 @@ def rank_program(g, core, T, topo):
 
     def block(src, r, buf, col, rsem):
         w = cnt[src][r]
-        o = loff(r, src)
+        o = loff[r][src]
         write(cores[r], T.land[:, o:o + w], buf[:, col:col + w], rsem)
 
     host0 = me - me % 8
@@ -77,16 +128,16 @@ def rank_program(g, core, T, topo):
         for c in chunks(me):
             if c[0] == lc:
                 cable(c)
-    if lc == 7:
+    if lc == neighbour(me):
         g.wait_ge(sem.hin, 16)
         for d in turn:
-            block(me, other0 + d, T.zs, zoff(me, other0 + d), sem.near)
-    if lc in (2, 3):
+            block(me, other0 + d, T.zs, zoff[me][other0 + d], sem.near)
+    if lc == 2 or lc == forward(me):
         src = partner(me)
         g.wait_ge(sem.fin, 16)
         for d in turn[1:] + turn[:1]:
             r = (host0 if lc == 2 else other0) + d
-            block(src, r, T.land, zoff(src, r) - cbase(src), sem.far)
+            block(src, r, T.land, zoff[src][r] - cbase(src), sem.far)
     if lc != 6:
         g.wait_ge(sem.sent, nsent[0])
         return
@@ -100,10 +151,10 @@ def rank_program(g, core, T, topo):
     for c in chunks(me):
         if c[0] == 6:
             cable(c)
-    a, b = zoff(me, other0), zoff(me, other0 + 8)
-    write(chip0 + 7, T.zs[:, a:b], T.zs[:, a:b], sem.hin)
+    a, b = zoff[me][other0], zoff[me][other0 + 8]
+    write(chip0 + neighbour(me), T.zs[:, a:b], T.zs[:, a:b], sem.hin)
     for d in turn[1:]:
-        block(me, host0 + d, T.zs, zoff(me, host0 + d), sem.near)
+        block(me, host0 + d, T.zs, zoff[me][host0 + d], sem.near)
     g.wait_ge(sem.sent, nsent[0])
 
     v = g.vector
@@ -127,14 +178,14 @@ def rank_program(g, core, T, topo):
     near0 = 16 * (me // 16)
     v.wait_ge(sem.gl, 16)
     v.wait_ge(sem.zl, 16)
-    weigh(T.zs, zoff(me, me), pos[me][me])
+    weigh(T.zs, zoff[me][me], pos[me][me])
     v.wait_ge(sem.near, 15 * 8)
     for e in range(near0, near0 + 16):
         if e != me:
-            weigh(T.land, loff(me, e), pos[e][me])
+            weigh(T.land, loff[me][e], pos[e][me])
     v.wait_ge(sem.far, 15 * 8 + 16)
     for e in range(16 - near0, 32 - near0):
-        weigh(T.land, loff(me, e), pos[e][me])
+        weigh(T.land, loff[me][e], pos[e][me])
     v.wait_ge(sem.vs, nmul[0])
     w = nt * nk
     v.tensor_tensor(T.ys[:], T.gs[:, 0:w:nk], T.gs[:, 1:w:nk], AluOpType.add).then_inc(sem.va, 1)

from concourse.mybir import AluOpType

SCRATCH = {
    "zs": ("sbuf", [128, 825], "float32"),
    "gs": ("sbuf", [128, 768], "float32"),
    "land": ("sbuf", [128, 768], "float32"),
    "ys": ("sbuf", [128, 256], "float32"),
}
SEMAPHORES = ["zl", "gl", "hin", "fin", "near", "far", "sent", "vs", "va", "vdone", "stored"]

CHIP, OFF = 0xFFFF, 0x00FF
CACHE = {}


def partner(s):
    return (3 - s // 8) * 8 + s % 8


def balance(cnt):
    n = len(cnt)

    def cost(swap):
        load = {}

        def wr(x, die, r, c):
            at = x
            if x % 2 != r % 2:
                load[("m", x, die)] = load.get(("m", x, die), 0) + c
                at = x ^ 1
            if at != r:
                load[("o", at, die)] = load.get(("o", at, die), 0) + c
                load[("i", r, die)] = load.get(("i", r, die), 0) + c

        for x in range(n):
            own, oth, s = x - x % 8, (x - x % 8) ^ 8, partner(x)
            for d in range(8):
                if own + d != x:
                    wr(x, 0, own + d, cnt[x][own + d])
                    wr(x, 1, own + d, cnt[s][own + d])
                wr(x, swap[x], oth + d, cnt[x][oth + d])
                wr(x, 1 - swap[x], oth + d, cnt[s][oth + d])
        return sum(v * v for v in load.values())

    swap = [0] * n
    best = cost(swap)
    better = True
    while better:
        better = False
        for x in range(n):
            swap[x] ^= 1
            c = cost(swap)
            if c < best:
                best, better = c, True
            else:
                swap[x] ^= 1
    return swap


def plan(T):
    if "plan" not in CACHE:
        n = len(T.cores)
        route, nt, nk = T.tables["ROUTE"], T.tables["T"], T.tables["K"]
        pos = [[[] for _ in range(n)] for _ in range(n)]
        for r in range(n):
            for t in range(nt):
                for k in range(nk):
                    pos[route[r][t][k]][r].append(t * nk + k)
        cnt = [[len(pos[e][r]) for r in range(n)] for e in range(n)]
        zoff = [[sum(cnt[e][:r]) for r in range(n + 1)] for e in range(n)]
        loff = [[sum(cnt[x][r] for x in range(e)) for e in range(n + 1)] for r in range(n)]
        CACHE["plan"] = (pos, cnt, zoff, loff, balance(cnt))
    return CACHE["plan"]


def rank_program(g, core, T, topo):
    cores = T.cores
    lc = core % 8
    if topo.chip(core) >= 8 or lc in (1, 5):
        return
    chip0 = core - lc
    me = T.rank_of(chip0 + 6)
    pos, cnt, zoff, loff, swap = plan(T)
    nt, nk = T.tables["T"], T.tables["K"]
    sem = T.sem

    def neighbour(s):
        return 3 if swap[s] else 7

    def forward(s):
        return 7 if swap[s] else 3

    def cbase(s):
        return zoff[s][16 * (1 - s // 16)]

    def chunks(s):
        far0 = 16 * (1 - s // 16)
        out = []
        for half, senders in ((far0, (0, 2)), (far0 + 8, (4, 6))):
            a, b = zoff[s][half], zoff[s][half + 8]
            to = 2 if half // 8 == partner(s) // 8 else forward(partner(s))
            out.append((senders[0], to, a, (a + b) // 2))
            out.append((senders[1], to, (a + b) // 2, b))
        return out

    nsent = [0]

    def write(dst, out_ap, in_ap, rsem):
        rid, pid = topo.addr(dst, core)
        mask = CHIP if dst - dst % 8 == chip0 else OFF
        g.remote_dma(out_ap, in_ap, rsem, sem.sent, pid, rid, mask)
        nsent[0] += 16 if mask == CHIP else 8

    def cable(c):
        a, b = c[2] - cbase(me), c[3] - cbase(me)
        write(cores[partner(me)] - 6 + c[1], T.land[:, a:b], T.zs[:, c[2]:c[3]], sem.fin)

    def block(src, r, buf, col, rsem):
        w = cnt[src][r]
        o = loff[r][src]
        write(cores[r], T.land[:, o:o + w], buf[:, col:col + w], rsem)

    host0 = me - me % 8
    other0 = host0 ^ 8
    turn = [(me % 8 + d) % 8 for d in range(8)]

    if lc in (0, 2, 4):
        g.wait_ge(sem.hin, 16)
        for c in chunks(me):
            if c[0] == lc:
                cable(c)
    if lc == neighbour(me):
        g.wait_ge(sem.hin, 16)
        for d in turn:
            block(me, other0 + d, T.zs, zoff[me][other0 + d], sem.near)
    if lc == 2 or lc == forward(me):
        src = partner(me)
        g.wait_ge(sem.fin, 16)
        for d in turn[1:] + turn[:1]:
            r = (host0 if lc == 2 else other0) + d
            block(src, r, T.land, zoff[src][r] - cbase(src), sem.far)
    if lc != 6:
        g.wait_ge(sem.sent, nsent[0])
        return

    g.sync.dma_start(T.zs[:], T.z[:]).then_inc(sem.zl, 16)
    g.scalar.dma_start(T.gs[:], T.g[:]).then_inc(sem.gl, 16)
    g.wait_ge(sem.zl, 16)
    for c in chunks(me):
        if c[0] != 6:
            write(chip0 + c[0], T.zs[:, c[2]:c[3]], T.zs[:, c[2]:c[3]], sem.hin)
    for c in chunks(me):
        if c[0] == 6:
            cable(c)
    a, b = zoff[me][other0], zoff[me][other0 + 8]
    write(chip0 + neighbour(me), T.zs[:, a:b], T.zs[:, a:b], sem.hin)
    for d in turn[1:]:
        block(me, host0 + d, T.zs, zoff[me][host0 + d], sem.near)
    g.wait_ge(sem.sent, nsent[0])

    v = g.vector
    nmul = [0]

    def weigh(buf, off, cols):
        i = 0
        while i < len(cols):
            j = i
            step = 1
            if i + 1 < len(cols):
                step = cols[i + 1] - cols[i]
                j = i + 1
                while j + 1 < len(cols) and cols[j + 1] - cols[j] == step:
                    j += 1
            sl = slice(cols[i], cols[j] + 1, step)
            v.tensor_tensor(T.gs[:, sl], buf[:, off + i:off + j + 1], T.gs[:, sl], AluOpType.mult).then_inc(sem.vs, 1)
            nmul[0] += 1
            i = j + 1

    near0 = 16 * (me // 16)
    v.wait_ge(sem.gl, 16)
    v.wait_ge(sem.zl, 16)
    weigh(T.zs, zoff[me][me], pos[me][me])
    v.wait_ge(sem.near, 15 * 8)
    for e in range(near0, near0 + 16):
        if e != me:
            weigh(T.land, loff[me][e], pos[e][me])
    v.wait_ge(sem.far, 15 * 8 + 16)
    for e in range(16 - near0, 32 - near0):
        weigh(T.land, loff[me][e], pos[e][me])
    v.wait_ge(sem.vs, nmul[0])
    w = nt * nk
    v.tensor_tensor(T.ys[:], T.gs[:, 0:w:nk], T.gs[:, 1:w:nk], AluOpType.add).then_inc(sem.va, 1)
    v.wait_ge(sem.va, 1)
    v.tensor_tensor(T.ys[:], T.ys[:], T.gs[:, 2:w:nk], AluOpType.add).then_inc(sem.vdone, 1)
    g.sync.wait_ge(sem.vdone, 1)
    g.sync.dma_start(T.y[:], T.ys[:]).then_inc(sem.stored, 16)
    g.sync.wait_ge(sem.stored, 16)
